import numpy as np
import ml_dtypes


def mxq(x, axis, fmt="e4m3"):
    dtype, down = {"e4m3": (ml_dtypes.float8_e4m3fn, 7), "e5m2": (ml_dtypes.float8_e5m2, 14)}[fmt]
    v = np.moveaxis(np.asarray(x, np.float32).astype(ml_dtypes.bfloat16).astype(np.float64), axis, -1)
    blocks = v.reshape(v.shape[:-1] + (-1, 32))
    amax = np.abs(blocks).max(-1, keepdims=True)
    byte = np.maximum(np.where(amax > 0, np.frexp(amax)[1] - 1 + 127, 0) - down, 1)
    scale = np.exp2(byte - 127.0)
    codes = (blocks / scale).astype(np.float32).astype(dtype).astype(np.float64)
    return np.moveaxis((codes * scale).reshape(v.shape), -1, axis)


WIDE = False


def mx_kscale(k):
    if not WIDE:
        return np.ones(k)
    levels = np.array([10, -10, 5, -5, 0])
    if k % 512:
        return np.exp2(np.random.permutation(np.resize(levels, k // 32))).repeat(32)
    a = np.empty((k // 512, 16))
    for p in range(k // 512):
        a[p, :8] = np.random.permutation(np.resize(levels, 8))
        for g in range(8):
            far = levels[np.abs(levels - a[p, g]) >= 10]
            a[p, g + 8] = far[np.random.randint(len(far))]
    return np.exp2(a.ravel()).repeat(32)


def f64(x):
    return np.asarray(x).astype(np.float64)


def striped(idx):
    return np.tile(idx.reshape(-1, 16).T, (8, 1)).astype(np.uint16)


def unstriped(offs):
    return offs[:16].T.reshape(-1).astype(np.int64)


E2M1 = np.array([0.0, 0.5, 1.0, 1.5, 2.0, 3.0, 4.0, 6.0, -0.0, -0.5, -1.0, -1.5, -2.0, -3.0, -4.0, -6.0])


def pack_fp4(w):
    k, n = w.shape
    w = f64(np.asarray(w, np.float32).astype(ml_dtypes.bfloat16)).reshape(k // 32, 32, n)
    amax = np.abs(w).max(1)
    mant, ex = np.frexp(amax / 6.0)
    byte = np.clip(np.where(amax > 0, np.where(mant > 0.5, ex, ex - 1) + 127, 1), 1, 254)
    scaled = (w * np.exp2(127.0 - byte)[:, None, :]).reshape(k, n).astype(np.float32)
    c = np.ascontiguousarray(scaled.reshape(k // 512, 128, 4, n).transpose(0, 1, 3, 2)).astype(ml_dtypes.float4_e2m1fn).view(np.uint8) & 0xF
    words = (c[..., 0::2] | (c[..., 1::2] << 4)).reshape(k // 512, 128, 2 * n)
    return np.ascontiguousarray(words), np.ascontiguousarray(byte.astype(np.uint8).reshape(k // 512, 16, n))


def unpack_fp4(words, scales):
    g, _, n = scales.shape
    words = np.ascontiguousarray(words).reshape(g, 128, n, 2)
    nib = np.empty((g, 128, n, 4), np.uint8)
    nib[..., 0::2] = words & 0xF
    nib[..., 1::2] = words >> 4
    vals = E2M1[nib] * np.repeat(np.exp2(scales.astype(np.float64) - 127.0), 8, axis=1)[..., None]
    return vals.transpose(0, 1, 3, 2).reshape(g * 512, n)


K, T, S, V, H, N = 1024, 2048, 512, 256, 512, 128


def setup_inputs():
    n = np.random.standard_normal
    s = mx_kscale(K)[:, None]
    u = mx_kscale(H)
    packed_xT = pack_fp4(n((K, T)) * s)
    return {
        "x_words": packed_xT[0],
        "x_scales": packed_xT[1],
        "w1": (n((K, H)) / np.sqrt(K) / s * u).astype(np.float32),
        "w2": (n((H, N)) / np.sqrt(3 * H) / u[:, None]).astype(np.float32),
        "w3": (n((H, N)) / np.sqrt(3 * H) / u[:, None]).astype(np.float32),
        "w4": (n((H, N)) / np.sqrt(3 * H) / u[:, None]).astype(np.float32),
        "offs": striped(np.random.permutation(T)[:S]),
        "pos1": striped(np.random.permutation(S)[:V]),
        "pos2": striped(np.random.permutation(S)[:V]),
        "pos3": striped(np.random.permutation(S)[:V]),
        "pos4": striped(np.random.permutation(S)[:V]),
    }


def reference(x_words, x_scales, w1, w2, w3, w4, offs, pos1, pos2, pos3, pos4):
    xq = unpack_fp4(x_words, x_scales)[:, unstriped(offs)]
    h = mxq(f64(w1), 0, "e4m3").T @ xq
    g0 = h[:, unstriped(pos1)]
    g1 = h[:, unstriped(pos2)]
    g2 = h[:, unstriped(pos3)]
    g3 = h[:, unstriped(pos4)]
    z1 = (g0 + g1 + g2 + g3) / 4
    z2 = np.maximum(np.maximum(np.maximum(g0, g1), g2), g3)
    z3 = np.minimum(np.minimum(np.minimum(g0, g1), g2), g3)
    return mxq(f64(w2), 0, "e4m3").T @ mxq(z1, 0, "e4m3") + mxq(f64(w3), 0, "e4m3").T @ mxq(z2, 0, "e4m3") + mxq(f64(w4), 0, "e4m3").T @ mxq(z3, 0, "e4m3")

@@ -1,0 +1,189 @@
+from contextlib import ExitStack
+
+import concourse.mybir as mybir
+from concourse.masks import make_identity
+
+K, T, S, V, H, N = 1024, 2048, 512, 256, 512, 128
+FLOPS = 2 * K * H * S + 3 * 2 * H * N * V
+
+F32 = mybir.dt.float32
+BF16 = mybir.dt.bfloat16
+I32 = mybir.dt.int32
+U32 = mybir.dt.uint32
+U16 = mybir.dt.uint16
+U8 = mybir.dt.uint8
+FP8X4 = mybir.dt.float8_e4m3fn_x4
+FP4X4 = mybir.dt.float4_e2m1fn_x4
+MAX = mybir.AluOpType.max
+MIN = mybir.AluOpType.min
+COPY = mybir.ActivationFunctionType.Copy
+
+P = 128
+PACK = 4
+PASSES = K // (P * PACK)
+D = 4
+
+
+def tile_picked_pna_none_p_kernel(
+    tc, x_words, x_scales, w1, w2, w3, w4, offs, pos1, pos2, pos3, pos4, out
+):
+    nc = tc.nc
+    with ExitStack() as ctx:
+        keep = ctx.enter_context(tc.tile_pool(name="keep", bufs=1))
+        ring = ctx.enter_context(tc.tile_pool(name="ring", bufs=3))
+        psum = ctx.enter_context(tc.psum_pool(name="psum", bufs=1))
+
+        words = [keep.tile([P, T], U16, name="words%d" % z, align_bytes=64) for z in range(PASSES)]
+        nc.sync.dma_start(words[0][:].bitcast(I32), x_words[0].bitcast(I32))
+        offsets = keep.tile([P, S // 16], U16, name="offsets")
+        nc.sync.dma_start(offsets[:], offs)
+        places = []
+        for d, pos in enumerate((pos1, pos2, pos3, pos4)):
+            place = keep.tile([P, V // 16], U16, name="places%d" % d)
+            nc.sync.dma_start(place[:], pos)
+            places.append(place)
+        nc.sync.dma_start(words[1][:].bitcast(I32), x_words[1].bitcast(I32))
+
+        planes = keep.tile([P, PASSES, T], U8, name="planes", align_bytes=64)
+        nc.vector.memset(planes[:].bitcast(I32), 0)
+        scale_rows = x_scales.bitcast(I32).rearrange("z (q j) c -> j q z c", j=4)
+        for j in range(4):
+            nc.scalar.dma_start(planes[:].bitcast(I32)[j:P:32], scale_rows[j])
+
+        ident16 = keep.tile([P, P], BF16, name="ident16")
+        make_identity(nc, ident16[:])
+        ident = keep.tile([P, P], F32, name="ident")
+        nc.scalar.activation(ident[:], ident16[:], COPY)
+        w1_rows = w1.rearrange("(z p j) c -> z p j c", p=P, j=PACK)
+        w1_raw = [keep.tile([P, PACK, H], F32, name="w1_raw0")]
+        nc.sync.dma_start(w1_raw[0][:], w1_rows[0])
+
+        x_codes = [keep.tile([P, S], U16, name="x_codes%d" % z, align_bytes=64) for z in range(PASSES)]
+        x_bytes = [keep.tile([P, S], U8, name="x_bytes%d" % z, align_bytes=64) for z in range(PASSES)]
+        for z in range(PASSES):
+            nc.vector.tensor_copy(x_codes[z][:], words[z][:].indirect(offsets[:]))
+        for z in range(PASSES):
+            nc.vector.tensor_copy(x_bytes[z][:], planes[:, z, :].indirect(offsets[:]))
+
+        w1_raw.append(keep.tile([P, PACK, H], F32, name="words0", align_bytes=64))
+        nc.sync.dma_start(w1_raw[1][:], w1_rows[1])
+        w_raw = keep.tile([P, 3, PACK, N], F32, name="words1", align_bytes=64)
+        for a, w in enumerate((w2, w3, w4)):
+            nc.sync.dma_start(w_raw[:, a], w.rearrange("(p j) n -> p j n", j=PACK))
+
+        w1_codes = [keep.tile([P, H], U32, name="w1_codes%d" % z, align_bytes=64) for z in range(PASSES)]
+        w1_scales = [keep.tile([P, H], U8, name="w1_scales%d" % z, align_bytes=64) for z in range(PASSES)]
+        h_banks = [psum.tile([P, S], F32, name="bank%d" % t) for t in range(PACK)]
+        h = [keep.tile([P, S], F32, name="h%d" % t) for t in range(PACK)]
+        for z in range(PASSES):
+            src = w1_raw[z][:].rearrange("p j (m u e) -> u p m j e", u=2, e=2)
+            for u in range(2):
+                on_vector = u != z if z == 0 else u == 0
+                tag = "planes" if (z, u) == (0, 1) else "w1_grouped%d%d" % (z, u)
+                grouped = keep.tile([P, 2 * P * PACK], BF16, name=tag, align_bytes=64)
+                dst = grouped[:].rearrange("p (e m j) -> p m j e", e=2, j=PACK)
+                if on_vector:
+                    nc.vector.tensor_copy(dst, src[u])
+                else:
+                    nc.scalar.copy(dst, src[u])
+                pieces = 2 if (z, u) == (1, 0) else 1
+                width = 2 * P // pieces
+                for i in range(pieces):
+                    cols = slice(2 * P * u + i * width, 2 * P * u + (i + 1) * width)
+                    nc.vector.quantize_mx(
+                        w1_codes[z][:, cols].bitcast(FP8X4),
+                        w1_scales[z][:, cols],
+                        grouped[:, i * width * PACK : (i + 1) * width * PACK],
+                    )
+            for t in range(PACK):
+                nc.tensor.matmul_mx(
+                    h_banks[t][:],
+                    lhsT=w1_codes[z][:, t * P : (t + 1) * P].bitcast(FP8X4),
+                    lhsT_scale=w1_scales[z][:, t * P : (t + 1) * P],
+                    rhs=x_codes[z][:].bitcast(FP4X4),
+                    rhs_scale=x_bytes[z][:],
+                    start=(z == 0),
+                    stop=(z == PASSES - 1),
+                )
+        for t in range(PACK):
+            nc.scalar.copy(h[t][:], h_banks[t][:])
+
+        w_grouped = keep.tile([P, 3 * N * PACK], BF16, name="w_grouped", align_bytes=64)
+        for a in range(3):
+            dst = w_grouped[:, a * N * PACK : (a + 1) * N * PACK]
+            nc.scalar.copy(
+                dst.rearrange("p (c i j) -> p c j i", i=4, j=PACK),
+                w_raw[:, a].rearrange("p j (c i) -> p c j i", i=4),
+            )
+        w_codes = keep.tile([P, 3 * N], U32, name="w_codes", align_bytes=64)
+        w_scales = keep.tile([P, 3 * N], U8, name="w_scales", align_bytes=64)
+        for lo, hi in ((0, 2 * N), (2 * N, 3 * N)):
+            nc.vector.quantize_mx(
+                w_codes[:, lo:hi].bitcast(FP8X4), w_scales[:, lo:hi], w_grouped[:, lo * PACK : hi * PACK]
+            )
+
+        halves = V // P
+        sums = [psum.tile([P, PACK, P], F32, name="sums%d" % b) for b in range(halves)]
+        rounded = []
+        for d in range(D):
+            g = ring.tile([P, PACK, V], F32, name="g")
+            for t in range(PACK):
+                nc.vector.tensor_copy(g[:, t, :], h[t][:].indirect(places[d][:]))
+                for b in range(halves):
+                    nc.tensor.matmul(
+                        sums[b][:, t, :],
+                        lhsT=g[:, t, b * P : (b + 1) * P],
+                        rhs=ident[:],
+                        is_transpose=True,
+                        start=(d == 0 and t == 0),
+                        stop=(d == D - 1 and t == PACK - 1),
+                    )
+            gb = keep.tile([P, V * PACK], BF16, name="rounded%d" % d, align_bytes=64)
+            nc.scalar.copy(
+                gb[:].rearrange("p (c i t) -> p c t i", i=4, t=PACK),
+                g[:].rearrange("p t (c i) -> p c t i", i=4),
+            )
+            rounded.append(gb)
+
+        z = [keep.tile([P, V * PACK], BF16, name="z%d" % a, align_bytes=64) for a in range(3)]
+        for b in range(halves):
+            mean_t = keep.tile([P, 2, P, 2], BF16, name="mean_t%d" % b, align_bytes=64)
+            nc.scalar.activation(
+                mean_t[:], sums[b][:].rearrange("v (u e) p -> v u p e", e=2), COPY, scale=1.0 / D
+            )
+            pairs = mean_t[:].rearrange("v u p e -> v (u p e)").bitcast(F32)
+            back = psum.tile([P, 2, P], F32, name="bank%d" % b)
+            for u in range(2):
+                nc.tensor.transpose(back[:, u, :], pairs[:, u * P : (u + 1) * P], ident[:])
+            nc.scalar.copy(
+                z[0][:, b * P * PACK : (b + 1) * P * PACK].bitcast(F32).rearrange("p (v u) -> p v u", u=2),
+                back[:].rearrange("p u v -> p v u"),
+            )
+
+        largest, smallest = rounded[0], rounded[0]
+        for d in range(1, D):
+            last = d == D - 1
+            hi = z[1] if last else keep.tile([P, V * PACK], BF16, name="largest%d" % d, align_bytes=64)
+            lo = z[2] if last else keep.tile([P, V * PACK], BF16, name="smallest%d" % d, align_bytes=64)
+            nc.vector.tensor_tensor(hi[:], largest[:], rounded[d][:], MAX)
+            nc.vector.tensor_tensor(lo[:], smallest[:], rounded[d][:], MIN)
+            largest, smallest = hi, lo
+
+        acc = psum.tile([P, V], F32, name="acc")
+        order = (1, 2, 0)
+        for a in order:
+            z_codes = keep.tile([P, V], U32, name="z_codes%d" % a, align_bytes=64)
+            z_scales = keep.tile([P, V], U8, name="z_scales%d" % a, align_bytes=64)
+            nc.vector.quantize_mx(z_codes[:].bitcast(FP8X4), z_scales[:], z[a][:])
+            nc.tensor.matmul_mx(
+                acc[:],
+                lhsT=w_codes[:, a * N : (a + 1) * N].bitcast(FP8X4),
+                lhsT_scale=w_scales[:, a * N : (a + 1) * N],
+                rhs=z_codes[:].bitcast(FP8X4),
+                rhs_scale=z_scales[:],
+                start=(a == order[0]),
+                stop=(a == order[-1]),
+            )
+        result = keep.tile([P, V], F32, name="result")
+        nc.vector.tensor_copy(result[:], acc[:])
+        nc.sync.dma_start(out, result[:])

@@ -22,6 +22,7 @@ P = 128
 PACK = 4
 PASSES = K // (P * PACK)
 D = 4
+VECTOR_ROWS = ((0, 0), (80, 64))
 
 
 def tile_picked_pna_none_p_kernel(
@@ -30,6 +31,7 @@ def tile_picked_pna_none_p_kernel(
     nc = tc.nc
     with ExitStack() as ctx:
         keep = ctx.enter_context(tc.tile_pool(name="keep", bufs=1))
+        shared = ctx.enter_context(tc.tile_pool(name="shared", bufs=1))
         ring = ctx.enter_context(tc.tile_pool(name="ring", bufs=3))
         psum = ctx.enter_context(tc.psum_pool(name="psum", bufs=1))
 
@@ -44,48 +46,52 @@ def tile_picked_pna_none_p_kernel(
             places.append(place)
         nc.sync.dma_start(words[1][:].bitcast(I32), x_words[1].bitcast(I32))
 
-        planes = keep.tile([P, PASSES, T], U8, name="planes", align_bytes=64)
-        nc.vector.memset(planes[:].bitcast(I32), 0)
-        scale_rows = x_scales.bitcast(I32).rearrange("z (q j) c -> j q z c", j=4)
-        for j in range(4):
-            nc.scalar.dma_start(planes[:].bitcast(I32)[j:P:32], scale_rows[j])
-
-        ident16 = keep.tile([P, P], BF16, name="ident16")
-        make_identity(nc, ident16[:])
-        ident = keep.tile([P, P], F32, name="ident")
-        nc.scalar.activation(ident[:], ident16[:], COPY)
         w1_rows = w1.rearrange("(z p j) c -> z p j c", p=P, j=PACK)
-        w1_raw = [keep.tile([P, PACK, H], F32, name="w1_raw0")]
-        nc.sync.dma_start(w1_raw[0][:], w1_rows[0])
+        w1_raw = [keep.tile([P, PACK, H], F32, name="w1_raw%d" % z) for z in range(PASSES)]
+        for z in range(PASSES):
+            nc.sync.dma_start(w1_raw[z][:], w1_rows[z])
+
+        planes = shared.tile([P, T], U8, name="planes", align_bytes=64, offset=2048)
+        nc.gpsimd.memset(planes[:].bitcast(I32), 0)
+        scale_rows = x_scales.bitcast(I32).rearrange("z (q j) c -> q z j c", j=4)
+        for q in range(4):
+            nc.gpsimd.dma_start(planes[:].bitcast(I32)[32 * q : 32 * q + 8], scale_rows[q])
+
+        ident = keep.tile([P, P], F32, name="ident")
+        make_identity(nc, ident[:])
 
         x_codes = [keep.tile([P, S], U16, name="x_codes%d" % z, align_bytes=64) for z in range(PASSES)]
         x_bytes = [keep.tile([P, S], U8, name="x_bytes%d" % z, align_bytes=64) for z in range(PASSES)]
+        nc.vector.memset(x_bytes[1][:].bitcast(I32), 0)
         for z in range(PASSES):
             nc.vector.tensor_copy(x_codes[z][:], words[z][:].indirect(offsets[:]))
-        for z in range(PASSES):
-            nc.vector.tensor_copy(x_bytes[z][:], planes[:, z, :].indirect(offsets[:]))
-
-        w1_raw.append(keep.tile([P, PACK, H], F32, name="words0", align_bytes=64))
-        nc.sync.dma_start(w1_raw[1][:], w1_rows[1])
-        w_raw = keep.tile([P, 3, PACK, N], F32, name="words1", align_bytes=64)
+        nc.vector.tensor_copy(x_bytes[0][:], planes[:].indirect(offsets[:]))
+        for j in range(4):
+            nc.sync.dma_start(x_bytes[1][:].bitcast(I32)[j:P:32], x_bytes[0][:].bitcast(I32)[4 + j : P : 32])
+        w_raw = shared.tile([P, 3, PACK, N], F32, name="w_raw", align_bytes=64, offset=2624)
         for a, w in enumerate((w2, w3, w4)):
             nc.sync.dma_start(w_raw[:, a], w.rearrange("(p j) n -> p j n", j=PACK))
 
         w1_codes = [keep.tile([P, H], U32, name="w1_codes%d" % z, align_bytes=64) for z in range(PASSES)]
-        w1_scales = [keep.tile([P, H], U8, name="w1_scales%d" % z, align_bytes=64) for z in range(PASSES)]
+        w1_scales = [
+            shared.tile([P, H], U8, name="w1_scales0", align_bytes=64, offset=2112),
+            keep.tile([P, H], U8, name="w1_scales1", align_bytes=64),
+        ]
         h_banks = [psum.tile([P, S], F32, name="bank%d" % t) for t in range(PACK)]
         h = [keep.tile([P, S], F32, name="h%d" % t) for t in range(PACK)]
-        for z in range(PASSES):
-            src = w1_raw[z][:].rearrange("p j (m u e) -> u p m j e", u=2, e=2)
-            for u in range(2):
-                on_vector = u != z if z == 0 else u == 0
-                tag = "planes" if (z, u) == (0, 1) else "w1_grouped%d%d" % (z, u)
-                grouped = keep.tile([P, 2 * P * PACK], BF16, name=tag, align_bytes=64)
-                dst = grouped[:].rearrange("p (e m j) -> p m j e", e=2, j=PACK)
-                if on_vector:
-                    nc.vector.tensor_copy(dst, src[u])
+        for u in range(2):
+            for z in range(PASSES):
+                src = w1_raw[z][:].rearrange("p j (m u e) -> p u m j e", u=2, e=2)[:, u]
+                if (z, u) == (1, 0):
+                    grouped = shared.tile([P, 2 * P * PACK], BF16, name="w1_late", align_bytes=64, offset=64)
                 else:
-                    nc.scalar.copy(dst, src[u])
+                    tag = "w1_even" if z == u else "w1_odd"
+                    grouped = keep.tile([P, 2 * P * PACK], BF16, name=tag, align_bytes=64)
+                dst = grouped[:].rearrange("p (e m j) -> p m j e", e=2, j=PACK)
+                cut = VECTOR_ROWS[z][u]
+                if cut:
+                    nc.vector.tensor_copy(dst[:, :cut], src[:, :cut])
+                nc.scalar.activation(dst[:, cut:], src[:, cut:], COPY)
                 pieces = 2 if (z, u) == (1, 0) else 1
                 width = 2 * P // pieces
                 for i in range(pieces):
@@ -95,16 +101,17 @@ def tile_picked_pna_none_p_kernel(
                         w1_scales[z][:, cols],
                         grouped[:, i * width * PACK : (i + 1) * width * PACK],
                     )
-            for t in range(PACK):
-                nc.tensor.matmul_mx(
-                    h_banks[t][:],
-                    lhsT=w1_codes[z][:, t * P : (t + 1) * P].bitcast(FP8X4),
-                    lhsT_scale=w1_scales[z][:, t * P : (t + 1) * P],
-                    rhs=x_codes[z][:].bitcast(FP4X4),
-                    rhs_scale=x_bytes[z][:],
-                    start=(z == 0),
-                    stop=(z == PASSES - 1),
-                )
+            for t in (2 * u, 2 * u + 1):
+                for z in range(PASSES):
+                    nc.tensor.matmul_mx(
+                        h_banks[t][:],
+                        lhsT=w1_codes[z][:, t * P : (t + 1) * P].bitcast(FP8X4),
+                        lhsT_scale=w1_scales[z][:, t * P : (t + 1) * P],
+                        rhs=x_codes[z][:].bitcast(FP4X4),
+                        rhs_scale=x_bytes[z][:],
+                        start=(z == 0),
+                        stop=(z == PASSES - 1),
+                    )
         for t in range(PACK):
             nc.scalar.copy(h[t][:], h_banks[t][:])
 

@@ -22,7 +22,6 @@ P = 128
 PACK = 4
 PASSES = K // (P * PACK)
 D = 4
-VECTOR_ROWS = ((0, 0), (80, 64))
 
 
 def tile_picked_pna_none_p_kernel(
@@ -31,96 +30,86 @@ def tile_picked_pna_none_p_kernel(
     nc = tc.nc
     with ExitStack() as ctx:
         keep = ctx.enter_context(tc.tile_pool(name="keep", bufs=1))
-        shared = ctx.enter_context(tc.tile_pool(name="shared", bufs=1))
         ring = ctx.enter_context(tc.tile_pool(name="ring", bufs=3))
         psum = ctx.enter_context(tc.psum_pool(name="psum", bufs=1))
 
-        words = [keep.tile([P, T], U16, name="words%d" % z, align_bytes=64) for z in range(PASSES)]
-        nc.sync.dma_start(words[0][:].bitcast(I32), x_words[0].bitcast(I32))
+        rows = keep.tile([P, T], U8, name="rows", align_bytes=64)
+        nc.sync.dma_start(rows[:].bitcast(I32)[0:32], x_scales.bitcast(I32).rearrange("z q c -> (z q) c"))
+        nc.vector.memset(rows[:].bitcast(I32)[32:64], 0)
+        nc.vector.memset(rows[:].bitcast(I32)[64:P], 0)
         offsets = keep.tile([P, S // 16], U16, name="offsets")
         nc.sync.dma_start(offsets[:], offs)
+        words = [keep.tile([P, T], U16, name="words%d" % z, align_bytes=64) for z in range(PASSES)]
+        nc.sync.dma_start(words[0][:].bitcast(I32), x_words[0].bitcast(I32))
         places = []
         for d, pos in enumerate((pos1, pos2, pos3, pos4)):
             place = keep.tile([P, V // 16], U16, name="places%d" % d)
             nc.sync.dma_start(place[:], pos)
             places.append(place)
         nc.sync.dma_start(words[1][:].bitcast(I32), x_words[1].bitcast(I32))
-
         w1_rows = w1.rearrange("(z p j) c -> z p j c", p=P, j=PACK)
-        w1_raw = [keep.tile([P, PACK, H], F32, name="w1_raw%d" % z) for z in range(PASSES)]
-        for z in range(PASSES):
-            nc.sync.dma_start(w1_raw[z][:], w1_rows[z])
-
-        planes = shared.tile([P, T], U8, name="planes", align_bytes=64, offset=2048)
-        nc.gpsimd.memset(planes[:].bitcast(I32), 0)
-        scale_rows = x_scales.bitcast(I32).rearrange("z (q j) c -> q z j c", j=4)
-        for q in range(4):
-            nc.gpsimd.dma_start(planes[:].bitcast(I32)[32 * q : 32 * q + 8], scale_rows[q])
+        w1_raw = [keep.tile([P, PACK, H], F32, name="w1_raw0")]
+        nc.sync.dma_start(w1_raw[0][:], w1_rows[0])
 
         ident = keep.tile([P, P], F32, name="ident")
         make_identity(nc, ident[:])
 
-        x_codes = [keep.tile([P, S], U16, name="x_codes%d" % z, align_bytes=64) for z in range(PASSES)]
+        picked_rows = keep.tile([P, S], U8, name="picked_rows", align_bytes=64)
+        nc.vector.tensor_copy(picked_rows[:], rows[:].indirect(offsets[:]))
         x_bytes = [keep.tile([P, S], U8, name="x_bytes%d" % z, align_bytes=64) for z in range(PASSES)]
-        nc.vector.memset(x_bytes[1][:].bitcast(I32), 0)
+        for z in range(PASSES):
+            nc.vector.memset(x_bytes[z][:].bitcast(I32), 0)
+            for q in range(4):
+                queue = nc.gpsimd if z == 1 and q >= 2 else nc.sync
+                queue.dma_start(
+                    x_bytes[z][:].bitcast(I32)[32 * q : 32 * q + 4],
+                    picked_rows[:].bitcast(I32)[16 * z + 4 * q : 16 * z + 4 * q + 4],
+                )
+        w1_raw.append(keep.tile([P, PACK, H], F32, name="rows", align_bytes=64))
+        nc.sync.dma_start(w1_raw[1][:], w1_rows[1])
+        x_codes = [keep.tile([P, S], U16, name="x_codes%d" % z, align_bytes=64) for z in range(PASSES)]
         for z in range(PASSES):
             nc.vector.tensor_copy(x_codes[z][:], words[z][:].indirect(offsets[:]))
-        nc.vector.tensor_copy(x_bytes[0][:], planes[:].indirect(offsets[:]))
-        for j in range(4):
-            nc.sync.dma_start(x_bytes[1][:].bitcast(I32)[j:P:32], x_bytes[0][:].bitcast(I32)[4 + j : P : 32])
-        w_raw = shared.tile([P, 3, PACK, N], F32, name="w_raw", align_bytes=64, offset=2624)
-        for a, w in enumerate((w2, w3, w4)):
-            nc.sync.dma_start(w_raw[:, a], w.rearrange("(p j) n -> p j n", j=PACK))
 
         w1_codes = [keep.tile([P, H], U32, name="w1_codes%d" % z, align_bytes=64) for z in range(PASSES)]
-        w1_scales = [
-            shared.tile([P, H], U8, name="w1_scales0", align_bytes=64, offset=2112),
-            keep.tile([P, H], U8, name="w1_scales1", align_bytes=64),
-        ]
+        w1_scales = [keep.tile([P, H], U8, name="w1_scales%d" % z, align_bytes=64) for z in range(PASSES)]
         h_banks = [psum.tile([P, S], F32, name="bank%d" % t) for t in range(PACK)]
         h = [keep.tile([P, S], F32, name="h%d" % t) for t in range(PACK)]
-        for u in range(2):
-            for z in range(PASSES):
-                src = w1_raw[z][:].rearrange("p j (m u e) -> p u m j e", u=2, e=2)[:, u]
-                if (z, u) == (1, 0):
-                    grouped = shared.tile([P, 2 * P * PACK], BF16, name="w1_late", align_bytes=64, offset=64)
+        for z in range(PASSES):
+            src = w1_raw[z][:].rearrange("p j (a t r) -> p t a j r", t=PACK, r=2)
+            for t in range(PACK):
+                grouped = keep.tile([P, P * PACK], BF16, name="w1_grouped%d%d" % (z, t), align_bytes=64)
+                dst = grouped[:].rearrange("p (a r j) -> p a j r", r=2, j=PACK)
+                if t % 2 == 0:
+                    nc.vector.tensor_copy(dst, src[:, t])
                 else:
-                    tag = "w1_even" if z == u else "w1_odd"
-                    grouped = keep.tile([P, 2 * P * PACK], BF16, name=tag, align_bytes=64)
-                dst = grouped[:].rearrange("p (e m j) -> p m j e", e=2, j=PACK)
-                cut = VECTOR_ROWS[z][u]
-                if cut:
-                    nc.vector.tensor_copy(dst[:, :cut], src[:, :cut])
-                nc.scalar.activation(dst[:, cut:], src[:, cut:], COPY)
-                pieces = 2 if (z, u) == (1, 0) else 1
-                width = 2 * P // pieces
-                for i in range(pieces):
-                    cols = slice(2 * P * u + i * width, 2 * P * u + (i + 1) * width)
-                    nc.vector.quantize_mx(
-                        w1_codes[z][:, cols].bitcast(FP8X4),
-                        w1_scales[z][:, cols],
-                        grouped[:, i * width * PACK : (i + 1) * width * PACK],
-                    )
-            for t in (2 * u, 2 * u + 1):
-                for z in range(PASSES):
-                    nc.tensor.matmul_mx(
-                        h_banks[t][:],
-                        lhsT=w1_codes[z][:, t * P : (t + 1) * P].bitcast(FP8X4),
-                        lhsT_scale=w1_scales[z][:, t * P : (t + 1) * P],
-                        rhs=x_codes[z][:].bitcast(FP4X4),
-                        rhs_scale=x_bytes[z][:],
-                        start=(z == 0),
-                        stop=(z == PASSES - 1),
-                    )
+                    nc.scalar.activation(dst, src[:, t], COPY)
+                cols = slice(t * P, (t + 1) * P)
+                nc.vector.quantize_mx(w1_codes[z][:, cols].bitcast(FP8X4), w1_scales[z][:, cols], grouped[:])
         for t in range(PACK):
+            cols = slice(t * P, (t + 1) * P)
+            for z in range(PASSES):
+                nc.tensor.matmul_mx(
+                    h_banks[t][:],
+                    lhsT=w1_codes[z][:, cols].bitcast(FP8X4),
+                    lhsT_scale=w1_scales[z][:, cols],
+                    rhs=x_codes[z][:].bitcast(FP4X4),
+                    rhs_scale=x_bytes[z][:],
+                    start=(z == 0),
+                    stop=(z == PASSES - 1),
+                )
             nc.scalar.copy(h[t][:], h_banks[t][:])
 
-        w_grouped = keep.tile([P, 3 * N * PACK], BF16, name="w_grouped", align_bytes=64)
+        w_raw = keep.tile([P, 3, PACK, N], F32, name="w1_raw0")
+        for a, w in enumerate((w2, w3, w4)):
+            for r in range(2):
+                nc.sync.dma_start(w_raw[r:P:2, a], w.rearrange("(a t r) n -> r a t n", t=PACK, r=2)[r])
+        w_grouped = keep.tile([P, 3 * N * PACK], BF16, name="w1_codes1", align_bytes=64)
         for a in range(3):
             dst = w_grouped[:, a * N * PACK : (a + 1) * N * PACK]
             nc.scalar.copy(
-                dst.rearrange("p (c i j) -> p c j i", i=4, j=PACK),
-                w_raw[:, a].rearrange("p j (c i) -> p c j i", i=4),
+                dst.rearrange("p (c i j) -> p c j i", i=2, j=PACK),
+                w_raw[:, a].rearrange("p j (c i) -> p c j i", i=2),
             )
         w_codes = keep.tile([P, 3 * N], U32, name="w_codes", align_bytes=64)
         w_scales = keep.tile([P, 3 * N], U8, name="w_scales", align_bytes=64)
@@ -133,23 +122,26 @@ def tile_picked_pna_none_p_kernel(
         sums = [psum.tile([P, PACK, P], F32, name="sums%d" % b) for b in range(halves)]
         rounded = []
         for d in range(D):
-            g = ring.tile([P, PACK, V], F32, name="g")
-            for t in range(PACK):
-                nc.vector.tensor_copy(g[:, t, :], h[t][:].indirect(places[d][:]))
-                for b in range(halves):
-                    nc.tensor.matmul(
-                        sums[b][:, t, :],
-                        lhsT=g[:, t, b * P : (b + 1) * P],
-                        rhs=ident[:],
-                        is_transpose=True,
-                        start=(d == 0 and t == 0),
-                        stop=(d == D - 1 and t == PACK - 1),
-                    )
             gb = keep.tile([P, V * PACK], BF16, name="rounded%d" % d, align_bytes=64)
-            nc.scalar.copy(
-                gb[:].rearrange("p (c i t) -> p c t i", i=4, t=PACK),
-                g[:].rearrange("p t (c i) -> p c t i", i=4),
-            )
+            width = P if d == D - 1 else V
+            for v0 in range(0, V, width):
+                g = ring.tile([P, PACK, width], F32, name="g")
+                for t in range(PACK):
+                    piece = places[d][:, v0 // 16 : (v0 + width) // 16]
+                    nc.vector.tensor_copy(g[:, t, :], h[t][:].indirect(piece))
+                    for c0 in range(0, width, P):
+                        nc.tensor.matmul(
+                            sums[(v0 + c0) // P][:, t, :],
+                            lhsT=g[:, t, c0 : c0 + P],
+                            rhs=ident[:],
+                            is_transpose=True,
+                            start=(d == 0 and t == 0),
+                            stop=(d == D - 1 and t == PACK - 1),
+                        )
+                nc.scalar.copy(
+                    gb[:, v0 * PACK : (v0 + width) * PACK].rearrange("p (c i t) -> p c t i", i=2, t=PACK),
+                    g[:].rearrange("p t (c i) -> p c t i", i=2),
+                )
             rounded.append(gb)
 
         z = [keep.tile([P, V * PACK], BF16, name="z%d" % a, align_bytes=64) for a in range(3)]
@@ -176,21 +168,35 @@ def tile_picked_pna_none_p_kernel(
             nc.vector.tensor_tensor(lo[:], smallest[:], rounded[d][:], MIN)
             largest, smallest = hi, lo
 
-        acc = psum.tile([P, V], F32, name="acc")
+        z_codes = [keep.tile([P, V], U32, name="z_codes%d" % a, align_bytes=64) for a in range(3)]
+        z_scales = [keep.tile([P, V], U8, name="z_scales%d" % a, align_bytes=64) for a in range(3)]
         order = (1, 2, 0)
         for a in order:
-            z_codes = keep.tile([P, V], U32, name="z_codes%d" % a, align_bytes=64)
-            z_scales = keep.tile([P, V], U8, name="z_scales%d" % a, align_bytes=64)
-            nc.vector.quantize_mx(z_codes[:].bitcast(FP8X4), z_scales[:], z[a][:])
-            nc.tensor.matmul_mx(
-                acc[:],
-                lhsT=w_codes[:, a * N : (a + 1) * N].bitcast(FP8X4),
-                lhsT_scale=w_scales[:, a * N : (a + 1) * N],
-                rhs=z_codes[:].bitcast(FP8X4),
-                rhs_scale=z_scales[:],
-                start=(a == order[0]),
-                stop=(a == order[-1]),
-            )
-        result = keep.tile([P, V], F32, name="result")
-        nc.vector.tensor_copy(result[:], acc[:])
-        nc.sync.dma_start(out, result[:])
+            width = P if a == order[-1] else V
+            for v0 in range(0, V, width):
+                cols = slice(v0, v0 + width)
+                nc.vector.quantize_mx(
+                    z_codes[a][:, cols].bitcast(FP8X4),
+                    z_scales[a][:, cols],
+                    z[a][:, v0 * PACK : (v0 + width) * PACK],
+                )
+        for b in range(halves):
+            cols = slice(b * P, (b + 1) * P)
+            acc = psum.tile([P, P], F32, name="bank%d" % (2 + b))
+            for a in order:
+                nc.tensor.matmul_mx(
+                    acc[:],
+                    lhsT=w_codes[:, a * N : (a + 1) * N].bitcast(FP8X4),
+                    lhsT_scale=w_scales[:, a * N : (a + 1) * N],
+                    rhs=z_codes[a][:, cols].bitcast(FP8X4),
+                    rhs_scale=z_scales[a][:, cols],
+                    start=(a == order[0]),
+                    stop=(a == order[-1]),
+                )
+            result = keep.tile([P, P], F32, name="result%d" % b)
+            if b == 0:
+                nc.scalar.copy(result[:], acc[:])
+                nc.scalar.dma_start(out[:, cols], result[:])
+            else:
+                nc.vector.tensor_copy(result[:], acc[:])
+                nc.sync.dma_start(out[:, cols], result[:])

@@ -30,7 +30,6 @@ def tile_picked_pna_none_p_kernel(
     nc = tc.nc
     with ExitStack() as ctx:
         keep = ctx.enter_context(tc.tile_pool(name="keep", bufs=1))
-        ring = ctx.enter_context(tc.tile_pool(name="ring", bufs=3))
         psum = ctx.enter_context(tc.psum_pool(name="psum", bufs=1))
 
         rows = keep.tile([P, T], U8, name="rows", align_bytes=64)
@@ -46,10 +45,10 @@ def tile_picked_pna_none_p_kernel(
             place = keep.tile([P, V // 16], U16, name="places%d" % d)
             nc.sync.dma_start(place[:], pos)
             places.append(place)
-        nc.sync.dma_start(words[1][:].bitcast(I32), x_words[1].bitcast(I32))
         w1_rows = w1.rearrange("(z p j) c -> z p j c", p=P, j=PACK)
-        w1_raw = [keep.tile([P, PACK, H], F32, name="w1_raw0")]
-        nc.sync.dma_start(w1_raw[0][:], w1_rows[0])
+        w1_first = keep.tile([P, PACK, H], F32, name="w1_first", align_bytes=64)
+        nc.sync.dma_start(w1_first[:], w1_rows[0])
+        nc.sync.dma_start(words[1][:].bitcast(I32), x_words[1].bitcast(I32))
 
         ident = keep.tile([P, P], F32, name="ident")
         make_identity(nc, ident[:])
@@ -57,75 +56,104 @@ def tile_picked_pna_none_p_kernel(
         picked_rows = keep.tile([P, S], U8, name="picked_rows", align_bytes=64)
         nc.vector.tensor_copy(picked_rows[:], rows[:].indirect(offsets[:]))
         x_bytes = [keep.tile([P, S], U8, name="x_bytes%d" % z, align_bytes=64) for z in range(PASSES)]
-        for z in range(PASSES):
-            nc.vector.memset(x_bytes[z][:].bitcast(I32), 0)
-            for q in range(4):
-                queue = nc.gpsimd if z == 1 and q >= 2 else nc.sync
-                queue.dma_start(
-                    x_bytes[z][:].bitcast(I32)[32 * q : 32 * q + 4],
-                    picked_rows[:].bitcast(I32)[16 * z + 4 * q : 16 * z + 4 * q + 4],
-                )
-        w1_raw.append(keep.tile([P, PACK, H], F32, name="rows", align_bytes=64))
-        nc.sync.dma_start(w1_raw[1][:], w1_rows[1])
-        x_codes = [keep.tile([P, S], U16, name="x_codes%d" % z, align_bytes=64) for z in range(PASSES)]
-        for z in range(PASSES):
-            nc.vector.tensor_copy(x_codes[z][:], words[z][:].indirect(offsets[:]))
+        nc.vector.memset(x_bytes[1][:].bitcast(I32), 0)
+        nc.vector.tensor_copy(x_bytes[0][:].bitcast(I32), picked_rows[:].bitcast(I32))
+
+        def move_scale_rows(queue, z, q):
+            queue.dma_start(
+                x_bytes[z][:].bitcast(I32)[32 * q : 32 * q + 4],
+                picked_rows[:].bitcast(I32)[16 * z + 4 * q : 16 * z + 4 * q + 4],
+            )
+
+        for q in (1, 2, 3):
+            move_scale_rows(nc.sync, 0, q)
+        w1_second = keep.tile([P, 2, PACK, H // 2], F32, name="rows", align_bytes=64)
+        nc.sync.dma_start(w1_second[:, 0], w1_rows[1][:, :, : H // 2])
+        for q in (0, 1):
+            move_scale_rows(nc.sync, 1, q)
+        nc.sync.dma_start(w1_second[:, 1], w1_rows[1][:, :, H // 2 :])
+        for q in (2, 3):
+            move_scale_rows(nc.sync, 1, q)
+        x_codes = [keep.tile([P, S], U16, name="x_codes0", align_bytes=64)]
+        nc.vector.tensor_copy(x_codes[0][:], words[0][:].indirect(offsets[:]))
 
         w1_codes = [keep.tile([P, H], U32, name="w1_codes%d" % z, align_bytes=64) for z in range(PASSES)]
         w1_scales = [keep.tile([P, H], U8, name="w1_scales%d" % z, align_bytes=64) for z in range(PASSES)]
-        h_banks = [psum.tile([P, S], F32, name="bank%d" % t) for t in range(PACK)]
         h = [keep.tile([P, S], F32, name="h%d" % t) for t in range(PACK)]
-        for z in range(PASSES):
-            src = w1_raw[z][:].rearrange("p j (a t r) -> p t a j r", t=PACK, r=2)
-            for t in range(PACK):
-                grouped = keep.tile([P, P * PACK], BF16, name="w1_grouped%d%d" % (z, t), align_bytes=64)
-                dst = grouped[:].rearrange("p (a r j) -> p a j r", r=2, j=PACK)
-                if t % 2 == 0:
-                    nc.vector.tensor_copy(dst, src[:, t])
-                else:
-                    nc.scalar.activation(dst, src[:, t], COPY)
-                cols = slice(t * P, (t + 1) * P)
-                nc.vector.quantize_mx(w1_codes[z][:, cols].bitcast(FP8X4), w1_scales[z][:, cols], grouped[:])
+
+        def quantise_w1(z, t0, t1, grouped):
+            cols = slice(t0 * P, t1 * P)
+            nc.vector.quantize_mx(w1_codes[z][:, cols].bitcast(FP8X4), w1_scales[z][:, cols], grouped)
+
+        src = w1_first[:].rearrange("p j (a t r) -> p t a j r", t=PACK, r=2)
+        for u in range(2):
+            grouped = keep.tile([P, 2 * H], BF16, name="w1_pair%d" % u, align_bytes=64)
+            dst = grouped[:].rearrange("p (t a r j) -> p t a j r", t=2, r=2, j=PACK)
+            if u == 0:
+                nc.vector.tensor_copy(dst[:, 0], src[:, 0])
+                nc.vector.tensor_copy(dst[:, 1], src[:, 1])
+                quantise_w1(0, 0, 1, grouped[:, 0:H])
+                quantise_w1(0, 1, 2, grouped[:, H : 2 * H])
+            else:
+                nc.scalar.copy(dst, src[:, 2:4])
+                quantise_w1(0, 2, 4, grouped[:])
+        x_codes.append(keep.tile([P, S], U16, name="w1_pair1", align_bytes=64))
+        nc.vector.tensor_copy(x_codes[1][:], words[1][:].indirect(offsets[:]))
+        grouped = keep.tile([P, H * PACK], BF16, name="w1_grouped", align_bytes=64)
+        dst = grouped[:].rearrange("p (t h a r j) -> p h t a j r", t=PACK, h=2, r=2, j=PACK)
+        src = [w1_second[:, half].rearrange("p j (a t r) -> p t a j r", t=PACK, r=2) for half in range(2)]
+        nc.scalar.copy(dst[:, 0], src[0])
+        nc.vector.tensor_copy(dst[:, 1, 0], src[1][:, 0])
+        nc.vector.tensor_copy(dst[:, 1, 1], src[1][:, 1])
+        quantise_w1(1, 0, 1, grouped[:, 0:H])
+        nc.vector.tensor_copy(dst[:, 1, 2:4], src[1][:, 2:4])
+        quantise_w1(1, 1, 2, grouped[:, H : 2 * H])
+        quantise_w1(1, 2, 4, grouped[:, 2 * H : 4 * H])
+        banks = 0
         for t in range(PACK):
             cols = slice(t * P, (t + 1) * P)
-            for z in range(PASSES):
-                nc.tensor.matmul_mx(
-                    h_banks[t][:],
-                    lhsT=w1_codes[z][:, cols].bitcast(FP8X4),
-                    lhsT_scale=w1_scales[z][:, cols],
-                    rhs=x_codes[z][:].bitcast(FP4X4),
-                    rhs_scale=x_bytes[z][:],
-                    start=(z == 0),
-                    stop=(z == PASSES - 1),
-                )
-            nc.scalar.copy(h[t][:], h_banks[t][:])
+            width = P if t == 0 else S
+            for s0 in range(0, S, width):
+                entries = slice(s0, s0 + width)
+                bank = psum.tile([P, width], F32, name="bank%d" % banks)
+                banks += 1
+                for z in range(PASSES):
+                    nc.tensor.matmul_mx(
+                        bank[:],
+                        lhsT=w1_codes[z][:, cols].bitcast(FP8X4),
+                        lhsT_scale=w1_scales[z][:, cols],
+                        rhs=x_codes[z][:, entries].bitcast(FP4X4),
+                        rhs_scale=x_bytes[z][:, entries],
+                        start=(z == 0),
+                        stop=(z == PASSES - 1),
+                    )
+                if (s0 // width) % 2 == 0:
+                    nc.scalar.copy(h[t][:, entries], bank[:])
+                else:
+                    nc.vector.tensor_copy(h[t][:, entries], bank[:])
 
-        w_raw = keep.tile([P, 3, PACK, N], F32, name="w1_raw0")
-        for a, w in enumerate((w2, w3, w4)):
+        w_raw = []
+        for tag, w in zip(("w1_first", "w1_pair0", "words0"), (w2, w3, w4)):
+            raw = keep.tile([P, PACK, N], F32, name=tag, align_bytes=64)
             for r in range(2):
-                nc.sync.dma_start(w_raw[r:P:2, a], w.rearrange("(a t r) n -> r a t n", t=PACK, r=2)[r])
+                nc.sync.dma_start(raw[r:P:2], w.rearrange("(a t r) n -> r a t n", t=PACK, r=2)[r])
+            w_raw.append(raw)
         w_grouped = keep.tile([P, 3 * N * PACK], BF16, name="w1_codes1", align_bytes=64)
         for a in range(3):
             dst = w_grouped[:, a * N * PACK : (a + 1) * N * PACK]
             nc.scalar.copy(
                 dst.rearrange("p (c i j) -> p c j i", i=2, j=PACK),
-                w_raw[:, a].rearrange("p j (c i) -> p c j i", i=2),
-            )
-        w_codes = keep.tile([P, 3 * N], U32, name="w_codes", align_bytes=64)
-        w_scales = keep.tile([P, 3 * N], U8, name="w_scales", align_bytes=64)
-        for lo, hi in ((0, 2 * N), (2 * N, 3 * N)):
-            nc.vector.quantize_mx(
-                w_codes[:, lo:hi].bitcast(FP8X4), w_scales[:, lo:hi], w_grouped[:, lo * PACK : hi * PACK]
+                w_raw[a][:].rearrange("p j (c i) -> p c j i", i=2),
             )
 
         halves = V // P
-        sums = [psum.tile([P, PACK, P], F32, name="sums%d" % b) for b in range(halves)]
+        sums = [psum.tile([P, PACK, P], F32, name=("bank7", "bank0")[b]) for b in range(halves)]
         rounded = []
         for d in range(D):
             gb = keep.tile([P, V * PACK], BF16, name="rounded%d" % d, align_bytes=64)
-            width = P if d == D - 1 else V
+            width = V
             for v0 in range(0, V, width):
-                g = ring.tile([P, PACK, width], F32, name="g")
+                g = keep.tile([P, PACK, width], F32, name=("g0", "g1", "w1_first", "w1_pair0")[d], align_bytes=64)
                 for t in range(PACK):
                     piece = places[d][:, v0 // 16 : (v0 + width) // 16]
                     nc.vector.tensor_copy(g[:, t, :], h[t][:].indirect(piece))
@@ -144,6 +172,13 @@ def tile_picked_pna_none_p_kernel(
                 )
             rounded.append(gb)
 
+        w_codes = keep.tile([P, 3 * N], U32, name="w_codes", align_bytes=64)
+        w_scales = keep.tile([P, 3 * N], U8, name="w_scales", align_bytes=64)
+        for lo, hi in ((0, 2 * N), (2 * N, 3 * N)):
+            nc.vector.quantize_mx(
+                w_codes[:, lo:hi].bitcast(FP8X4), w_scales[:, lo:hi], w_grouped[:, lo * PACK : hi * PACK]
+            )
+
         z = [keep.tile([P, V * PACK], BF16, name="z%d" % a, align_bytes=64) for a in range(3)]
         for b in range(halves):
             mean_t = keep.tile([P, 2, P, 2], BF16, name="mean_t%d" % b, align_bytes=64)
@@ -151,7 +186,7 @@ def tile_picked_pna_none_p_kernel(
                 mean_t[:], sums[b][:].rearrange("v (u e) p -> v u p e", e=2), COPY, scale=1.0 / D
             )
             pairs = mean_t[:].rearrange("v u p e -> v (u p e)").bitcast(F32)
-            back = psum.tile([P, 2, P], F32, name="bank%d" % b)
+            back = psum.tile([P, 2, P], F32, name="bank%d" % (1 + b))
             for u in range(2):
                 nc.tensor.transpose(back[:, u, :], pairs[:, u * P : (u + 1) * P], ident[:])
             nc.scalar.copy(
@@ -182,7 +217,7 @@ def tile_picked_pna_none_p_kernel(
                 )
         for b in range(halves):
             cols = slice(b * P, (b + 1) * P)
-            acc = psum.tile([P, P], F32, name="bank%d" % (2 + b))
+            acc = psum.tile([P, P], F32, name="bank%d" % (3 + b))
             for a in order:
                 nc.tensor.matmul_mx(
                     acc[:],

@@ -106,7 +106,7 @@ def tile_picked_pna_none_p_kernel(
         nc.vector.tensor_copy(dst[:, 1, 0], src[1][:, 0])
         nc.vector.tensor_copy(dst[:, 1, 1], src[1][:, 1])
         quantise_w1(1, 0, 1, grouped[:, 0:H])
-        nc.vector.tensor_copy(dst[:, 1, 2:4], src[1][:, 2:4])
+        nc.scalar.copy(dst[:, 1, 2:4], src[1][:, 2:4])
         quantise_w1(1, 1, 2, grouped[:, H : 2 * H])
         quantise_w1(1, 2, 4, grouped[:, 2 * H : 4 * H])
         banks = 0
@@ -142,8 +142,8 @@ def tile_picked_pna_none_p_kernel(
         for a in range(3):
             dst = w_grouped[:, a * N * PACK : (a + 1) * N * PACK]
             nc.scalar.copy(
-                dst.rearrange("p (c i j) -> p c j i", i=2, j=PACK),
-                w_raw[a][:].rearrange("p j (c i) -> p c j i", i=2),
+                dst.rearrange("p (c i j) -> p c j i", i=4, j=PACK),
+                w_raw[a][:].rearrange("p j (c i) -> p c j i", i=4),
             )
 
         halves = V // P
@@ -167,8 +167,8 @@ def tile_picked_pna_none_p_kernel(
                             stop=(d == D - 1 and t == PACK - 1),
                         )
                 nc.scalar.copy(
-                    gb[:, v0 * PACK : (v0 + width) * PACK].rearrange("p (c i t) -> p c t i", i=2, t=PACK),
-                    g[:].rearrange("p t (c i) -> p c t i", i=2),
+                    gb[:, v0 * PACK : (v0 + width) * PACK].rearrange("p (c i t) -> p c t i", i=4, t=PACK),
+                    g[:].rearrange("p t (c i) -> p c t i", i=4),
                 )
             rounded.append(gb)
 
@@ -182,16 +182,20 @@ def tile_picked_pna_none_p_kernel(
         z = [keep.tile([P, V * PACK], BF16, name="z%d" % a, align_bytes=64) for a in range(3)]
         for b in range(halves):
             mean_t = keep.tile([P, 2, P, 2], BF16, name="mean_t%d" % b, align_bytes=64)
-            nc.scalar.activation(
-                mean_t[:], sums[b][:].rearrange("v (u e) p -> v u p e", e=2), COPY, scale=1.0 / D
-            )
+            for u in range(2):
+                nc.scalar.activation(
+                    mean_t[:, u].rearrange("v (c i) e -> v c e i", i=4),
+                    sums[b][:, 2 * u : 2 * u + 2].rearrange("v e (c i) -> v c e i", i=4),
+                    COPY,
+                    scale=1.0 / D,
+                )
             pairs = mean_t[:].rearrange("v u p e -> v (u p e)").bitcast(F32)
             back = psum.tile([P, 2, P], F32, name="bank%d" % (1 + b))
             for u in range(2):
                 nc.tensor.transpose(back[:, u, :], pairs[:, u * P : (u + 1) * P], ident[:])
             nc.scalar.copy(
-                z[0][:, b * P * PACK : (b + 1) * P * PACK].bitcast(F32).rearrange("p (v u) -> p v u", u=2),
-                back[:].rearrange("p u v -> p v u"),
+                z[0][:, b * P * PACK : (b + 1) * P * PACK].bitcast(F32).rearrange("p (c i u) -> p c u i", i=2, u=2),
+                back[:].rearrange("p u (c i) -> p c u i", i=2),
             )
 
         largest, smallest = rounded[0], rounded[0]

@@ -67,13 +67,12 @@ def tile_picked_pna_none_p_kernel(
 
         for q in (1, 2, 3):
             move_scale_rows(nc.sync, 0, q)
-        w1_second = keep.tile([P, 2, PACK, H // 2], F32, name="rows", align_bytes=64)
-        nc.sync.dma_start(w1_second[:, 0], w1_rows[1][:, :, : H // 2])
         for q in (0, 1):
             move_scale_rows(nc.sync, 1, q)
-        nc.sync.dma_start(w1_second[:, 1], w1_rows[1][:, :, H // 2 :])
+        w1_second = keep.tile([P, PACK, H], F32, name="rows", align_bytes=64)
+        nc.sync.dma_start(w1_second[:], w1_rows[1])
         for q in (2, 3):
-            move_scale_rows(nc.sync, 1, q)
+            move_scale_rows(nc.gpsimd, 1, q)
         x_codes = [keep.tile([P, S], U16, name="x_codes0", align_bytes=64)]
         nc.vector.tensor_copy(x_codes[0][:], words[0][:].indirect(offsets[:]))
 
@@ -100,13 +99,12 @@ def tile_picked_pna_none_p_kernel(
         x_codes.append(keep.tile([P, S], U16, name="w1_pair1", align_bytes=64))
         nc.vector.tensor_copy(x_codes[1][:], words[1][:].indirect(offsets[:]))
         grouped = keep.tile([P, H * PACK], BF16, name="w1_grouped", align_bytes=64)
-        dst = grouped[:].rearrange("p (t h a r j) -> p h t a j r", t=PACK, h=2, r=2, j=PACK)
-        src = [w1_second[:, half].rearrange("p j (a t r) -> p t a j r", t=PACK, r=2) for half in range(2)]
-        nc.scalar.copy(dst[:, 0], src[0])
-        nc.vector.tensor_copy(dst[:, 1, 0], src[1][:, 0])
-        nc.vector.tensor_copy(dst[:, 1, 1], src[1][:, 1])
+        dst = grouped[:].rearrange("p (t a r j) -> p t a j r", t=PACK, r=2, j=PACK)
+        src = w1_second[:].rearrange("p j (a t r) -> p t a j r", t=PACK, r=2)
+        nc.vector.tensor_copy(dst[:, 0], src[:, 0])
+        nc.vector.tensor_copy(dst[:, 1], src[:, 1])
         quantise_w1(1, 0, 1, grouped[:, 0:H])
-        nc.scalar.copy(dst[:, 1, 2:4], src[1][:, 2:4])
+        nc.scalar.copy(dst[:, 2:4], src[:, 2:4])
         quantise_w1(1, 1, 2, grouped[:, H : 2 * H])
         quantise_w1(1, 2, 4, grouped[:, 2 * H : 4 * H])
         banks = 0
@@ -138,12 +136,12 @@ def tile_picked_pna_none_p_kernel(
             for r in range(2):
                 nc.sync.dma_start(raw[r:P:2], w.rearrange("(a t r) n -> r a t n", t=PACK, r=2)[r])
             w_raw.append(raw)
-        w_grouped = keep.tile([P, 3 * N * PACK], BF16, name="w1_codes1", align_bytes=64)
-        for a in range(3):
-            dst = w_grouped[:, a * N * PACK : (a + 1) * N * PACK]
+        w34_grouped = keep.tile([P, 2, N * PACK], BF16, name="w1_codes1", align_bytes=64)
+        mean_w2 = keep.tile([P, 3, P * PACK], BF16, name="w1_pair1", align_bytes=64)
+        for raw, dst in zip(w_raw, (mean_w2[:, 0], w34_grouped[:, 0], w34_grouped[:, 1])):
             nc.scalar.copy(
                 dst.rearrange("p (c i j) -> p c j i", i=4, j=PACK),
-                w_raw[a][:].rearrange("p j (c i) -> p c j i", i=4),
+                raw[:].rearrange("p j (c i) -> p c j i", i=4),
             )
 
         halves = V // P
@@ -172,14 +170,6 @@ def tile_picked_pna_none_p_kernel(
                 )
             rounded.append(gb)
 
-        w_codes = keep.tile([P, 3 * N], U32, name="w_codes", align_bytes=64)
-        w_scales = keep.tile([P, 3 * N], U8, name="w_scales", align_bytes=64)
-        for lo, hi in ((0, 2 * N), (2 * N, 3 * N)):
-            nc.vector.quantize_mx(
-                w_codes[:, lo:hi].bitcast(FP8X4), w_scales[:, lo:hi], w_grouped[:, lo * PACK : hi * PACK]
-            )
-
-        z = [keep.tile([P, V * PACK], BF16, name="z%d" % a, align_bytes=64) for a in range(3)]
         for b in range(halves):
             mean_t = keep.tile([P, 2, P, 2], BF16, name="mean_t%d" % b, align_bytes=64)
             for u in range(2):
@@ -194,43 +184,50 @@ def tile_picked_pna_none_p_kernel(
             for u in range(2):
                 nc.tensor.transpose(back[:, u, :], pairs[:, u * P : (u + 1) * P], ident[:])
             nc.scalar.copy(
-                z[0][:, b * P * PACK : (b + 1) * P * PACK].bitcast(F32).rearrange("p (c i u) -> p c u i", i=2, u=2),
+                mean_w2[:, 1 + b].bitcast(F32).rearrange("p (c i u) -> p c u i", i=2, u=2),
                 back[:].rearrange("p u (c i) -> p c u i", i=2),
             )
 
-        largest, smallest = rounded[0], rounded[0]
+        extremes = keep.tile([P, 2, V * PACK], BF16, name="extremes", align_bytes=64)
+        largest, smallest = rounded[0][:], rounded[0][:]
         for d in range(1, D):
-            last = d == D - 1
-            hi = z[1] if last else keep.tile([P, V * PACK], BF16, name="largest%d" % d, align_bytes=64)
-            lo = z[2] if last else keep.tile([P, V * PACK], BF16, name="smallest%d" % d, align_bytes=64)
-            nc.vector.tensor_tensor(hi[:], largest[:], rounded[d][:], MAX)
-            nc.vector.tensor_tensor(lo[:], smallest[:], rounded[d][:], MIN)
+            if d == D - 1:
+                hi, lo = extremes[:, 0], extremes[:, 1]
+            else:
+                hi = keep.tile([P, V * PACK], BF16, name="largest%d" % d, align_bytes=64)[:]
+                lo = keep.tile([P, V * PACK], BF16, name="smallest%d" % d, align_bytes=64)[:]
+            nc.vector.tensor_tensor(hi, largest, rounded[d][:], MAX)
+            nc.vector.tensor_tensor(lo, smallest, rounded[d][:], MIN)
             largest, smallest = hi, lo
 
-        z_codes = [keep.tile([P, V], U32, name="z_codes%d" % a, align_bytes=64) for a in range(3)]
-        z_scales = [keep.tile([P, V], U8, name="z_scales%d" % a, align_bytes=64) for a in range(3)]
-        order = (1, 2, 0)
-        for a in order:
-            width = P if a == order[-1] else V
-            for v0 in range(0, V, width):
-                cols = slice(v0, v0 + width)
-                nc.vector.quantize_mx(
-                    z_codes[a][:, cols].bitcast(FP8X4),
-                    z_scales[a][:, cols],
-                    z[a][:, v0 * PACK : (v0 + width) * PACK],
-                )
+        def quantise(values, width, tag):
+            codes = keep.tile([P, width], U32, name=tag, align_bytes=64)
+            scales = keep.tile([P, width], U8, name=tag + "_scales", align_bytes=64)
+            nc.vector.quantize_mx(codes[:].bitcast(FP8X4), scales[:], values)
+            return codes, scales
+
+        w34 = quantise(w34_grouped[:].rearrange("p a c -> p (a c)"), 2 * N, "w34")
+        z2 = quantise(extremes[:, 0], V, "z2")
+        z3 = quantise(extremes[:, 1], V, "z3")
+        w2_z1 = quantise(mean_w2[:, 0:2].rearrange("p a c -> p (a c)"), N + P, "w2_z1")
+        z1_last = quantise(mean_w2[:, 2], P, "z1_last")
         for b in range(halves):
             cols = slice(b * P, (b + 1) * P)
             acc = psum.tile([P, P], F32, name="bank%d" % (3 + b))
-            for a in order:
+            passes = (
+                (w34, 0, z2, b * P),
+                (w34, N, z3, b * P),
+                (w2_z1, 0, w2_z1, N) if b == 0 else (w2_z1, 0, z1_last, 0),
+            )
+            for a, (w, m0, zq, v0) in enumerate(passes):
                 nc.tensor.matmul_mx(
                     acc[:],
-                    lhsT=w_codes[:, a * N : (a + 1) * N].bitcast(FP8X4),
-                    lhsT_scale=w_scales[:, a * N : (a + 1) * N],
-                    rhs=z_codes[a][:, cols].bitcast(FP8X4),
-                    rhs_scale=z_scales[a][:, cols],
-                    start=(a == order[0]),
-                    stop=(a == order[-1]),
+                    lhsT=w[0][:, m0 : m0 + N].bitcast(FP8X4),
+                    lhsT_scale=w[1][:, m0 : m0 + N],
+                    rhs=zq[0][:, v0 : v0 + P].bitcast(FP8X4),
+                    rhs_scale=zq[1][:, v0 : v0 + P],
+                    start=(a == 0),
+                    stop=(a == 2),
                 )
             result = keep.tile([P, P], F32, name="result%d" % b)
             if b == 0:

@@ -136,39 +136,50 @@ def tile_picked_pna_none_p_kernel(
             for r in range(2):
                 nc.sync.dma_start(raw[r:P:2], w.rearrange("(a t r) n -> r a t n", t=PACK, r=2)[r])
             w_raw.append(raw)
-        w34_grouped = keep.tile([P, 2, N * PACK], BF16, name="w1_codes1", align_bytes=64)
-        mean_w2 = keep.tile([P, 3, P * PACK], BF16, name="w1_pair1", align_bytes=64)
-        for raw, dst in zip(w_raw, (mean_w2[:, 0], w34_grouped[:, 0], w34_grouped[:, 1])):
-            nc.scalar.copy(
-                dst.rearrange("p (c i j) -> p c j i", i=4, j=PACK),
-                raw[:].rearrange("p j (c i) -> p c j i", i=4),
-            )
+        w34_grouped = keep.tile([P, 2, N * PACK], BF16, name="w34_grouped", align_bytes=64)
+        mean_w2 = keep.tile([P, 3, P * PACK], BF16, name="mean_w2", align_bytes=64)
 
         halves = V // P
         sums = [psum.tile([P, PACK, P], F32, name=("bank7", "bank0")[b]) for b in range(halves)]
-        rounded = []
+        extremes = keep.tile([P, 2, V * PACK], BF16, name="extremes", align_bytes=64)
         for d in range(D):
-            gb = keep.tile([P, V * PACK], BF16, name="rounded%d" % d, align_bytes=64)
-            width = V
-            for v0 in range(0, V, width):
-                g = keep.tile([P, PACK, width], F32, name=("g0", "g1", "w1_first", "w1_pair0")[d], align_bytes=64)
-                for t in range(PACK):
-                    piece = places[d][:, v0 // 16 : (v0 + width) // 16]
-                    nc.vector.tensor_copy(g[:, t, :], h[t][:].indirect(piece))
-                    for c0 in range(0, width, P):
-                        nc.tensor.matmul(
-                            sums[(v0 + c0) // P][:, t, :],
-                            lhsT=g[:, t, c0 : c0 + P],
-                            rhs=ident[:],
-                            is_transpose=True,
-                            start=(d == 0 and t == 0),
-                            stop=(d == D - 1 and t == PACK - 1),
-                        )
-                nc.scalar.copy(
-                    gb[:, v0 * PACK : (v0 + width) * PACK].rearrange("p (c i t) -> p c t i", i=4, t=PACK),
-                    g[:].rearrange("p t (c i) -> p c t i", i=4),
-                )
-            rounded.append(gb)
+            g = keep.tile([P, PACK, V], F32, name=("g0", "g1", "w1_codes1", "w1_pair1")[d], align_bytes=64)
+            for t in range(PACK):
+                if d == 0 or (d == 1 and t == PACK - 1):
+                    nc.vector.tensor_copy(g[:, t, :], h[t][:].indirect(places[d][:]))
+                else:
+                    nc.scalar.activation(g[:, t, :], h[t][:].indirect(places[d][:]), COPY)
+                for b in range(halves):
+                    nc.tensor.matmul(
+                        sums[b][:, t, :],
+                        lhsT=g[:, t, b * P : (b + 1) * P],
+                        rhs=ident[:],
+                        is_transpose=True,
+                        start=(d == 0 and t == 0),
+                        stop=(d == D - 1 and t == PACK - 1),
+                    )
+            gb = keep.tile([P, V * PACK], BF16, name="rounded%d" % min(d, 1), align_bytes=64)
+            nc.vector.tensor_copy(
+                gb[:].rearrange("p (c i t) -> p c t i", i=4, t=PACK),
+                g[:].rearrange("p t (c i) -> p c t i", i=4),
+            )
+            if d == 0:
+                largest, smallest = gb[:], gb[:]
+                continue
+            if d == D - 1:
+                hi, lo = extremes[:, 0], extremes[:, 1]
+            else:
+                hi = keep.tile([P, V * PACK], BF16, name="largest%d" % d, align_bytes=64)[:]
+                lo = keep.tile([P, V * PACK], BF16, name="smallest%d" % d, align_bytes=64)[:]
+            nc.vector.tensor_tensor(hi, largest, gb[:], MAX)
+            nc.vector.tensor_tensor(lo, smallest, gb[:], MIN)
+            largest, smallest = hi, lo
+            if d == 1:
+                for raw, dst in zip(w_raw, (mean_w2[:, 0], w34_grouped[:, 0], w34_grouped[:, 1])):
+                    nc.vector.tensor_copy(
+                        dst.rearrange("p (c i j) -> p c j i", i=4, j=PACK),
+                        raw[:].rearrange("p j (c i) -> p c j i", i=4),
+                    )
 
         for b in range(halves):
             mean_t = keep.tile([P, 2, P, 2], BF16, name="mean_t%d" % b, align_bytes=64)
@@ -188,20 +199,8 @@ def tile_picked_pna_none_p_kernel(
                 back[:].rearrange("p u (c i) -> p c u i", i=2),
             )
 
-        extremes = keep.tile([P, 2, V * PACK], BF16, name="extremes", align_bytes=64)
-        largest, smallest = rounded[0][:], rounded[0][:]
-        for d in range(1, D):
-            if d == D - 1:
-                hi, lo = extremes[:, 0], extremes[:, 1]
-            else:
-                hi = keep.tile([P, V * PACK], BF16, name="largest%d" % d, align_bytes=64)[:]
-                lo = keep.tile([P, V * PACK], BF16, name="smallest%d" % d, align_bytes=64)[:]
-            nc.vector.tensor_tensor(hi, largest, rounded[d][:], MAX)
-            nc.vector.tensor_tensor(lo, smallest, rounded[d][:], MIN)
-            largest, smallest = hi, lo
-
-        def quantise(values, width, tag):
-            codes = keep.tile([P, width], U32, name=tag, align_bytes=64)
+        def quantise(values, width, tag, over=None):
+            codes = keep.tile([P, width], U32, name=over or tag, align_bytes=64)
             scales = keep.tile([P, width], U8, name=tag + "_scales", align_bytes=64)
             nc.vector.quantize_mx(codes[:].bitcast(FP8X4), scales[:], values)
             return codes, scales
@@ -209,8 +208,8 @@ def tile_picked_pna_none_p_kernel(
         w34 = quantise(w34_grouped[:].rearrange("p a c -> p (a c)"), 2 * N, "w34")
         z2 = quantise(extremes[:, 0], V, "z2")
         z3 = quantise(extremes[:, 1], V, "z3")
-        w2_z1 = quantise(mean_w2[:, 0:2].rearrange("p a c -> p (a c)"), N + P, "w2_z1")
-        z1_last = quantise(mean_w2[:, 2], P, "z1_last")
+        w2_z1 = quantise(mean_w2[:, 0:2].rearrange("p a c -> p (a c)"), N + P, "w2_z1", "largest2")
+        z1_last = quantise(mean_w2[:, 2], P, "z1_last", "smallest2")
         for b in range(halves):
             cols = slice(b * P, (b + 1) * P)
             acc = psum.tile([P, P], F32, name="bank%d" % (3 + b))

@@ -33,7 +33,7 @@ def tile_picked_pna_none_p_kernel(
         psum = ctx.enter_context(tc.psum_pool(name="psum", bufs=1))
 
         rows = keep.tile([P, T], U8, name="rows", align_bytes=64)
-        nc.sync.dma_start(rows[:].bitcast(I32)[0:32], x_scales.bitcast(I32).rearrange("z q c -> (z q) c"))
+        nc.sync.dma_start(rows[:].bitcast(I32)[0:32], x_scales.bitcast(I32).rearrange("z q c -> q z c"))
         nc.vector.memset(rows[:].bitcast(I32)[32:64], 0)
         nc.vector.memset(rows[:].bitcast(I32)[64:P], 0)
         offsets = keep.tile([P, S // 16], U16, name="offsets")
@@ -55,30 +55,24 @@ def tile_picked_pna_none_p_kernel(
 
         picked_rows = keep.tile([P, S], U8, name="picked_rows", align_bytes=64)
         nc.vector.tensor_copy(picked_rows[:], rows[:].indirect(offsets[:]))
-        x_bytes = [keep.tile([P, S], U8, name="x_bytes%d" % z, align_bytes=64) for z in range(PASSES)]
-        nc.vector.memset(x_bytes[1][:].bitcast(I32), 0)
-        nc.vector.tensor_copy(x_bytes[0][:].bitcast(I32), picked_rows[:].bitcast(I32))
-
-        def move_scale_rows(queue, z, q):
-            queue.dma_start(
-                x_bytes[z][:].bitcast(I32)[32 * q : 32 * q + 4],
-                picked_rows[:].bitcast(I32)[16 * z + 4 * q : 16 * z + 4 * q + 4],
+        x_bytes = keep.tile([P, PASSES * S], U8, name="x_bytes", align_bytes=64)
+        nc.vector.memset(x_bytes[:].bitcast(I32), 0)
+        for q in range(4):
+            nc.sync.dma_start(
+                x_bytes[:].bitcast(I32)[32 * q : 32 * q + 4], picked_rows[:].bitcast(I32)[8 * q : 8 * q + 8]
             )
-
-        for q in (1, 2, 3):
-            move_scale_rows(nc.sync, 0, q)
-        for q in (0, 1):
-            move_scale_rows(nc.sync, 1, q)
-        w1_second = keep.tile([P, PACK, H], F32, name="rows", align_bytes=64)
-        nc.sync.dma_start(w1_second[:], w1_rows[1])
-        for q in (2, 3):
-            move_scale_rows(nc.gpsimd, 1, q)
+        w1_second = []
+        for e, tag in enumerate(("rows", "words0")):
+            half = keep.tile([P, PACK, H // 2], F32, name=tag, align_bytes=64)
+            w1_second.append(half)
+        nc.sync.dma_start(w1_second[0][:], w1_rows[1][:, :, : H // 2])
         x_codes = [keep.tile([P, S], U16, name="x_codes0", align_bytes=64)]
         nc.vector.tensor_copy(x_codes[0][:], words[0][:].indirect(offsets[:]))
+        nc.sync.dma_start(w1_second[1][:], w1_rows[1][:, :, H // 2 :])
 
         w1_codes = [keep.tile([P, H], U32, name="w1_codes%d" % z, align_bytes=64) for z in range(PASSES)]
         w1_scales = [keep.tile([P, H], U8, name="w1_scales%d" % z, align_bytes=64) for z in range(PASSES)]
-        h = [keep.tile([P, S], F32, name="h%d" % t) for t in range(PACK)]
+        h = [keep.tile([P, S], F32, name="h%d" % t, align_bytes=64) for t in range(PACK)]
 
         def quantise_w1(z, t0, t1, grouped):
             cols = slice(t0 * P, t1 * P)
@@ -99,12 +93,14 @@ def tile_picked_pna_none_p_kernel(
         x_codes.append(keep.tile([P, S], U16, name="w1_pair1", align_bytes=64))
         nc.vector.tensor_copy(x_codes[1][:], words[1][:].indirect(offsets[:]))
         grouped = keep.tile([P, H * PACK], BF16, name="w1_grouped", align_bytes=64)
-        dst = grouped[:].rearrange("p (t a r j) -> p t a j r", t=PACK, r=2, j=PACK)
-        src = w1_second[:].rearrange("p j (a t r) -> p t a j r", t=PACK, r=2)
-        nc.vector.tensor_copy(dst[:, 0], src[:, 0])
-        nc.vector.tensor_copy(dst[:, 1], src[:, 1])
+        dst = grouped[:].rearrange("p (t e a r j) -> p e t a j r", t=PACK, e=2, r=2, j=PACK)
+        src = [half[:].rearrange("p j (a t r) -> p t a j r", t=PACK, r=2) for half in w1_second]
+        nc.vector.tensor_copy(dst[:, 0, 0:2], src[0][:, 0:2])
+        nc.scalar.copy(dst[:, 0, 2:4], src[0][:, 2:4])
+        nc.vector.tensor_copy(dst[:, 1, 0], src[1][:, 0])
+        nc.vector.tensor_copy(dst[:, 1, 1], src[1][:, 1])
         quantise_w1(1, 0, 1, grouped[:, 0:H])
-        nc.scalar.copy(dst[:, 2:4], src[:, 2:4])
+        nc.scalar.copy(dst[:, 1, 2:4], src[1][:, 2:4])
         quantise_w1(1, 1, 2, grouped[:, H : 2 * H])
         quantise_w1(1, 2, 4, grouped[:, 2 * H : 4 * H])
         banks = 0
@@ -121,7 +117,7 @@ def tile_picked_pna_none_p_kernel(
                         lhsT=w1_codes[z][:, cols].bitcast(FP8X4),
                         lhsT_scale=w1_scales[z][:, cols],
                         rhs=x_codes[z][:, entries].bitcast(FP4X4),
-                        rhs_scale=x_bytes[z][:, entries],
+                        rhs_scale=x_bytes[:, z * S + s0 : z * S + s0 + width],
                         start=(z == 0),
                         stop=(z == PASSES - 1),
                     )
@@ -131,13 +127,12 @@ def tile_picked_pna_none_p_kernel(
                     nc.vector.tensor_copy(h[t][:, entries], bank[:])
 
         w_raw = []
-        for tag, w in zip(("w1_first", "w1_pair0", "words0"), (w2, w3, w4)):
+        for tag, w in zip(("w1_first", "w1_pair0", "words1"), (w2, w3, w4)):
             raw = keep.tile([P, PACK, N], F32, name=tag, align_bytes=64)
             for r in range(2):
                 nc.sync.dma_start(raw[r:P:2], w.rearrange("(a t r) n -> r a t n", t=PACK, r=2)[r])
             w_raw.append(raw)
         w34_grouped = keep.tile([P, 2, N * PACK], BF16, name="w34_grouped", align_bytes=64)
-        mean_w2 = keep.tile([P, 3, P * PACK], BF16, name="mean_w2", align_bytes=64)
 
         halves = V // P
         sums = [psum.tile([P, PACK, P], F32, name=("bank7", "bank0")[b]) for b in range(halves)]
@@ -175,12 +170,17 @@ def tile_picked_pna_none_p_kernel(
             nc.vector.tensor_tensor(lo, smallest, gb[:], MIN)
             largest, smallest = hi, lo
             if d == 1:
-                for raw, dst in zip(w_raw, (mean_w2[:, 0], w34_grouped[:, 0], w34_grouped[:, 1])):
+                for raw, dst in zip(w_raw[1:], (w34_grouped[:, 0], w34_grouped[:, 1])):
                     nc.vector.tensor_copy(
                         dst.rearrange("p (c i j) -> p c j i", i=4, j=PACK),
                         raw[:].rearrange("p j (c i) -> p c j i", i=4),
                     )
 
+        mean_w2 = keep.tile([P, 3, P * PACK], BF16, name="h3", align_bytes=64)
+        nc.scalar.copy(
+            mean_w2[:, 0].rearrange("p (c i j) -> p c j i", i=4, j=PACK),
+            w_raw[0][:].rearrange("p j (c i) -> p c j i", i=4),
+        )
         for b in range(halves):
             mean_t = keep.tile([P, 2, P, 2], BF16, name="mean_t%d" % b, align_bytes=64)
             for u in range(2):

@@ -132,15 +132,20 @@ def tile_picked_pna_none_p_kernel(
             for r in range(2):
                 nc.sync.dma_start(raw[r:P:2], w.rearrange("(a t r) n -> r a t n", t=PACK, r=2)[r])
             w_raw.append(raw)
-        w34_grouped = keep.tile([P, 2, N * PACK], BF16, name="w34_grouped", align_bytes=64)
+
+        def quantise(values, width, tag, over=None):
+            codes = keep.tile([P, width], U32, name=over or tag, align_bytes=64)
+            scales = keep.tile([P, width], U8, name=tag + "_scales", align_bytes=64)
+            nc.vector.quantize_mx(codes[:].bitcast(FP8X4), scales[:], values)
+            return codes, scales
 
         halves = V // P
         sums = [psum.tile([P, PACK, P], F32, name=("bank7", "bank0")[b]) for b in range(halves)]
-        extremes = keep.tile([P, 2, V * PACK], BF16, name="extremes", align_bytes=64)
-        for d in range(D):
-            g = keep.tile([P, PACK, V], F32, name=("g0", "g1", "w1_codes1", "w1_pair1")[d], align_bytes=64)
+
+        def gather_list(d, tag):
+            g = keep.tile([P, PACK, V], F32, name=tag, align_bytes=64)
             for t in range(PACK):
-                if d == 0 or (d == 1 and t == PACK - 1):
+                if d == 0 or (d == 1 and t >= PACK - 2):
                     nc.vector.tensor_copy(g[:, t, :], h[t][:].indirect(places[d][:]))
                 else:
                     nc.scalar.activation(g[:, t, :], h[t][:].indirect(places[d][:]), COPY)
@@ -153,28 +158,41 @@ def tile_picked_pna_none_p_kernel(
                         start=(d == 0 and t == 0),
                         stop=(d == D - 1 and t == PACK - 1),
                     )
-            gb = keep.tile([P, V * PACK], BF16, name="rounded%d" % min(d, 1), align_bytes=64)
+            return g
+
+        def round_list(g, tag):
+            rounded = keep.tile([P, V * PACK], BF16, name=tag, align_bytes=64)
             nc.vector.tensor_copy(
-                gb[:].rearrange("p (c i t) -> p c t i", i=4, t=PACK),
+                rounded[:].rearrange("p (c i t) -> p c t i", i=4, t=PACK),
                 g[:].rearrange("p t (c i) -> p c t i", i=4),
             )
-            if d == 0:
-                largest, smallest = gb[:], gb[:]
-                continue
-            if d == D - 1:
-                hi, lo = extremes[:, 0], extremes[:, 1]
-            else:
-                hi = keep.tile([P, V * PACK], BF16, name="largest%d" % d, align_bytes=64)[:]
-                lo = keep.tile([P, V * PACK], BF16, name="smallest%d" % d, align_bytes=64)[:]
-            nc.vector.tensor_tensor(hi, largest, gb[:], MAX)
-            nc.vector.tensor_tensor(lo, smallest, gb[:], MIN)
-            largest, smallest = hi, lo
-            if d == 1:
-                for raw, dst in zip(w_raw[1:], (w34_grouped[:, 0], w34_grouped[:, 1])):
-                    nc.vector.tensor_copy(
-                        dst.rearrange("p (c i j) -> p c j i", i=4, j=PACK),
-                        raw[:].rearrange("p j (c i) -> p c j i", i=4),
-                    )
+            return rounded
+
+        def round_w(dst, raw):
+            nc.vector.tensor_copy(
+                dst.rearrange("p (c i j) -> p c j i", i=4, j=PACK),
+                raw[:].rearrange("p j (c i) -> p c j i", i=4),
+            )
+
+        def extremes(largest, smallest, rounded, step):
+            hi = keep.tile([P, V * PACK], BF16, name="largest%d" % step, align_bytes=64)
+            lo = keep.tile([P, V * PACK], BF16, name="smallest%d" % step, align_bytes=64)
+            nc.vector.tensor_tensor(hi[:], largest[:], rounded[:], MAX)
+            nc.vector.tensor_tensor(lo[:], smallest[:], rounded[:], MIN)
+            return hi, lo
+
+        gathered = [gather_list(0, "g0"), gather_list(1, "g1")]
+        first = round_list(gathered[0], "rounded0")
+        second = round_list(gathered[1], "rounded1")
+        w34_grouped = keep.tile([P, 2, N * PACK], BF16, name="g0", align_bytes=64)
+        round_w(w34_grouped[:, 0], w_raw[1])
+        hi, lo = extremes(first, first, second, 1)
+        round_w(w34_grouped[:, 1], w_raw[2])
+        third = round_list(gather_list(2, "w1_codes1"), "rounded1")
+        w34 = quantise(w34_grouped[:].rearrange("p a c -> p (a c)"), 2 * N, "w34")
+        hi, lo = extremes(hi, lo, third, 2)
+        fourth = round_list(gather_list(3, "w1_pair1"), "largest1")
+        hi, lo = extremes(hi, lo, fourth, 3)
 
         mean_w2 = keep.tile([P, 3, P * PACK], BF16, name="h3", align_bytes=64)
         nc.scalar.copy(
@@ -199,15 +217,8 @@ def tile_picked_pna_none_p_kernel(
                 back[:].rearrange("p u (c i) -> p c u i", i=2),
             )
 
-        def quantise(values, width, tag, over=None):
-            codes = keep.tile([P, width], U32, name=over or tag, align_bytes=64)
-            scales = keep.tile([P, width], U8, name=tag + "_scales", align_bytes=64)
-            nc.vector.quantize_mx(codes[:].bitcast(FP8X4), scales[:], values)
-            return codes, scales
-
-        w34 = quantise(w34_grouped[:].rearrange("p a c -> p (a c)"), 2 * N, "w34")
-        z2 = quantise(extremes[:, 0], V, "z2")
-        z3 = quantise(extremes[:, 1], V, "z3")
+        z2 = quantise(hi[:], V, "z2")
+        z3 = quantise(lo[:], V, "z3")
         w2_z1 = quantise(mean_w2[:, 0:2].rearrange("p a c -> p (a c)"), N + P, "w2_z1", "largest2")
         z1_last = quantise(mean_w2[:, 2], P, "z1_last", "smallest2")
         for b in range(halves):

@@ -104,6 +104,7 @@ def tile_picked_pna_none_p_kernel(
         quantise_w1(1, 1, 2, grouped[:, H : 2 * H])
         quantise_w1(1, 2, 4, grouped[:, 2 * H : 4 * H])
         banks = 0
+        full = []
         for t in range(PACK):
             cols = slice(t * P, (t + 1) * P)
             width = P if t == 0 else S
@@ -121,10 +122,12 @@ def tile_picked_pna_none_p_kernel(
                         start=(z == 0),
                         stop=(z == PASSES - 1),
                     )
-                if (s0 // width) % 2 == 0:
-                    nc.scalar.copy(h[t][:, entries], bank[:])
-                else:
+                if t > 0:
+                    full.append(bank)
+                elif (s0 // width) % 2 == 0:
                     nc.vector.tensor_copy(h[t][:, entries], bank[:])
+                else:
+                    nc.scalar.copy(h[t][:, entries], bank[:])
 
         w_raw = []
         for tag, w in zip(("w1_first", "w1_pair0", "words1"), (w2, w3, w4)):
@@ -142,23 +145,23 @@ def tile_picked_pna_none_p_kernel(
         halves = V // P
         sums = [psum.tile([P, PACK, P], F32, name=("bank7", "bank0")[b]) for b in range(halves)]
 
-        def gather_list(d, tag):
-            g = keep.tile([P, PACK, V], F32, name=tag, align_bytes=64)
-            for t in range(PACK):
-                if d == 0 or (d == 1 and t >= PACK - 2):
-                    nc.vector.tensor_copy(g[:, t, :], h[t][:].indirect(places[d][:]))
-                else:
-                    nc.scalar.activation(g[:, t, :], h[t][:].indirect(places[d][:]), COPY)
-                for b in range(halves):
-                    nc.tensor.matmul(
-                        sums[b][:, t, :],
-                        lhsT=g[:, t, b * P : (b + 1) * P],
-                        rhs=ident[:],
-                        is_transpose=True,
-                        start=(d == 0 and t == 0),
-                        stop=(d == D - 1 and t == PACK - 1),
-                    )
-            return g
+        turned = []
+
+        def gather(g, d, t, on_vector=False):
+            if on_vector:
+                nc.vector.tensor_copy(g[:, t, :], h[t][:].indirect(places[d][:]))
+            else:
+                nc.scalar.activation(g[:, t, :], h[t][:].indirect(places[d][:]), COPY)
+            for b in range(halves):
+                nc.tensor.matmul(
+                    sums[b][:, t, :],
+                    lhsT=g[:, t, b * P : (b + 1) * P],
+                    rhs=ident[:],
+                    is_transpose=True,
+                    start=(len(turned) == 0),
+                    stop=(len(turned) == D * PACK - 1),
+                )
+            turned.append((d, t))
 
         def round_list(g, tag):
             rounded = keep.tile([P, V * PACK], BF16, name=tag, align_bytes=64)
@@ -181,17 +184,32 @@ def tile_picked_pna_none_p_kernel(
             nc.vector.tensor_tensor(lo[:], smallest[:], rounded[:], MIN)
             return hi, lo
 
-        gathered = [gather_list(0, "g0"), gather_list(1, "g1")]
+        gathered = [
+            keep.tile([P, PACK, V], F32, name=tag, align_bytes=64) for tag in ("g0", "g1", "g2", "w1_pair1")
+        ]
+        gather(gathered[0], 0, 0, on_vector=True)
+        gather(gathered[1], 1, 0)
+        gather(gathered[2], 2, 0, on_vector=True)
+        for t in range(1, PACK):
+            nc.scalar.copy(h[t][:], full[t - 1][:])
+            gather(gathered[0], 0, t, on_vector=True)
+        gather(gathered[1], 1, 1)
+        gather(gathered[1], 1, 3, on_vector=True)
+        gather(gathered[1], 1, 2)
         first = round_list(gathered[0], "rounded0")
         second = round_list(gathered[1], "rounded1")
         w34_grouped = keep.tile([P, 2, N * PACK], BF16, name="g0", align_bytes=64)
         round_w(w34_grouped[:, 0], w_raw[1])
         hi, lo = extremes(first, first, second, 1)
         round_w(w34_grouped[:, 1], w_raw[2])
-        third = round_list(gather_list(2, "w1_codes1"), "rounded1")
+        for t in range(1, PACK):
+            gather(gathered[2], 2, t)
+        third = round_list(gathered[2], "rounded1")
         w34 = quantise(w34_grouped[:].rearrange("p a c -> p (a c)"), 2 * N, "w34")
         hi, lo = extremes(hi, lo, third, 2)
-        fourth = round_list(gather_list(3, "w1_pair1"), "largest1")
+        for t in range(PACK):
+            gather(gathered[3], 3, t)
+        fourth = round_list(gathered[3], "largest1")
         hi, lo = extremes(hi, lo, fourth, 3)
 
         mean_w2 = keep.tile([P, 3, P * PACK], BF16, name="h3", align_bytes=64)

@@ -260,7 +260,6 @@ def tile_picked_pna_none_p_kernel(
             result = keep.tile([P, P], F32, name="result%d" % b)
             if b == 0:
                 nc.scalar.copy(result[:], acc[:])
-                nc.scalar.dma_start(out[:, cols], result[:])
             else:
                 nc.vector.tensor_copy(result[:], acc[:])
-                nc.sync.dma_start(out[:, cols], result[:])
+            nc.sync.dma_start(out[:, cols], result[:])

@@ -201,15 +201,15 @@ def tile_picked_pna_none_p_kernel(
         w34_grouped = keep.tile([P, 2, N * PACK], BF16, name="g0", align_bytes=64)
         round_w(w34_grouped[:, 0], w_raw[1])
         hi, lo = extremes(first, first, second, 1)
-        round_w(w34_grouped[:, 1], w_raw[2])
         for t in range(1, PACK):
             gather(gathered[2], 2, t)
-        third = round_list(gathered[2], "rounded1")
-        w34 = quantise(w34_grouped[:].rearrange("p a c -> p (a c)"), 2 * N, "w34")
+        third = round_list(gathered[2], "g1")
+        round_w(w34_grouped[:, 1], w_raw[2])
         hi, lo = extremes(hi, lo, third, 2)
         for t in range(PACK):
             gather(gathered[3], 3, t)
         fourth = round_list(gathered[3], "largest1")
+        w34 = quantise(w34_grouped[:].rearrange("p a c -> p (a c)"), 2 * N, "w34")
         hi, lo = extremes(hi, lo, fourth, 3)
 
         mean_w2 = keep.tile([P, 3, P * PACK], BF16, name="h3", align_bytes=64)

@@ -22,6 +22,7 @@ P = 128
 PACK = 4
 PASSES = K // (P * PACK)
 D = 4
+VECTOR_SHARE = 48
 
 
 def tile_picked_pna_none_p_kernel(
@@ -70,13 +71,20 @@ def tile_picked_pna_none_p_kernel(
         nc.vector.tensor_copy(x_codes[0][:], words[0][:].indirect(offsets[:]))
         nc.sync.dma_start(w1_second[1][:], w1_rows[1][:, :, H // 2 :])
 
-        w1_codes = [keep.tile([P, H], U32, name="w1_codes%d" % z, align_bytes=64) for z in range(PASSES)]
-        w1_scales = [keep.tile([P, H], U8, name="w1_scales%d" % z, align_bytes=64) for z in range(PASSES)]
+        spans = ((0, 1), (1, 2), (2, 4))
+        w1_codes, w1_scales = {}, {}
+        for z in range(PASSES):
+            for t0, t1 in spans:
+                codes = keep.tile([P, (t1 - t0) * P], U32, name="w1_codes%d%d" % (z, t0), align_bytes=64)
+                scales = keep.tile([P, (t1 - t0) * P], U8, name="w1_scales%d%d" % (z, t0), align_bytes=64)
+                w1_codes[z, t0, t1], w1_scales[z, t0, t1] = codes[:], scales[:]
+                for t in range(t0, t1):
+                    cols = slice((t - t0) * P, (t - t0 + 1) * P)
+                    w1_codes[z, t], w1_scales[z, t] = codes[:, cols], scales[:, cols]
         h = [keep.tile([P, S], F32, name="h%d" % t, align_bytes=64) for t in range(PACK)]
 
         def quantise_w1(z, t0, t1, grouped):
-            cols = slice(t0 * P, t1 * P)
-            nc.vector.quantize_mx(w1_codes[z][:, cols].bitcast(FP8X4), w1_scales[z][:, cols], grouped)
+            nc.vector.quantize_mx(w1_codes[z, t0, t1].bitcast(FP8X4), w1_scales[z, t0, t1], grouped)
 
         src = w1_first[:].rearrange("p j (a t r) -> p t a j r", t=PACK, r=2)
         for u in range(2):
@@ -106,7 +114,6 @@ def tile_picked_pna_none_p_kernel(
         banks = 0
         full = []
         for t in range(PACK):
-            cols = slice(t * P, (t + 1) * P)
             width = P if t == 0 else S
             for s0 in range(0, S, width):
                 entries = slice(s0, s0 + width)
@@ -115,8 +122,8 @@ def tile_picked_pna_none_p_kernel(
                 for z in range(PASSES):
                     nc.tensor.matmul_mx(
                         bank[:],
-                        lhsT=w1_codes[z][:, cols].bitcast(FP8X4),
-                        lhsT_scale=w1_scales[z][:, cols],
+                        lhsT=w1_codes[z, t].bitcast(FP8X4),
+                        lhsT_scale=w1_scales[z, t],
                         rhs=x_codes[z][:, entries].bitcast(FP4X4),
                         rhs_scale=x_bytes[:, z * S + s0 : z * S + s0 + width],
                         start=(z == 0),
@@ -130,7 +137,7 @@ def tile_picked_pna_none_p_kernel(
                     nc.scalar.copy(h[t][:, entries], bank[:])
 
         w_raw = []
-        for tag, w in zip(("w1_first", "w1_pair0", "words1"), (w2, w3, w4)):
+        for tag, w in zip(("picked_rows", "w1_pair0", "words1"), (w3, w4, w2)):
             raw = keep.tile([P, PACK, N], F32, name=tag, align_bytes=64)
             for r in range(2):
                 nc.sync.dma_start(raw[r:P:2], w.rearrange("(a t r) n -> r a t n", t=PACK, r=2)[r])
@@ -143,9 +150,9 @@ def tile_picked_pna_none_p_kernel(
             return codes, scales
 
         halves = V // P
-        sums = [psum.tile([P, PACK, P], F32, name=("bank7", "bank0")[b]) for b in range(halves)]
+        sums = [psum.tile([P, halves, 2, P], F32, name=("bank7", "bank0")[u]) for u in range(2)]
 
-        turned = []
+        turned = [[], []]
 
         def gather(g, d, t, on_vector=False):
             if on_vector:
@@ -154,14 +161,14 @@ def tile_picked_pna_none_p_kernel(
                 nc.scalar.activation(g[:, t, :], h[t][:].indirect(places[d][:]), COPY)
             for b in range(halves):
                 nc.tensor.matmul(
-                    sums[b][:, t, :],
+                    sums[t // 2][:, b, t % 2, :],
                     lhsT=g[:, t, b * P : (b + 1) * P],
                     rhs=ident[:],
                     is_transpose=True,
-                    start=(len(turned) == 0),
-                    stop=(len(turned) == D * PACK - 1),
+                    start=(len(turned[t // 2]) == 0),
+                    stop=(len(turned[t // 2]) == 2 * D * halves - 1),
                 )
-            turned.append((d, t))
+                turned[t // 2].append((d, t, b))
 
         def round_list(g, tag):
             rounded = keep.tile([P, V * PACK], BF16, name=tag, align_bytes=64)
@@ -187,6 +194,8 @@ def tile_picked_pna_none_p_kernel(
         gathered = [
             keep.tile([P, PACK, V], F32, name=tag, align_bytes=64) for tag in ("g0", "g1", "g2", "w1_pair1")
         ]
+        w3_grouped = keep.tile([P, N * PACK], BF16, name="w1_codes10", align_bytes=64)
+        round_w(w3_grouped[:], w_raw[0])
         gather(gathered[0], 0, 0, on_vector=True)
         gather(gathered[1], 1, 0)
         gather(gathered[2], 2, 0, on_vector=True)
@@ -198,41 +207,49 @@ def tile_picked_pna_none_p_kernel(
         gather(gathered[1], 1, 2)
         first = round_list(gathered[0], "rounded0")
         second = round_list(gathered[1], "rounded1")
-        w34_grouped = keep.tile([P, 2, N * PACK], BF16, name="g0", align_bytes=64)
-        round_w(w34_grouped[:, 0], w_raw[1])
+        w4_grouped = keep.tile([P, N * PACK], BF16, name="g0", align_bytes=64)
+        round_w(w4_grouped[:], w_raw[1])
         hi, lo = extremes(first, first, second, 1)
         for t in range(1, PACK):
             gather(gathered[2], 2, t)
         third = round_list(gathered[2], "g1")
-        round_w(w34_grouped[:, 1], w_raw[2])
+        w3q = quantise(w3_grouped[:], N, "w3q", "rounded1")
+        w4q = quantise(w4_grouped[:], N, "w4q", "rounded0")
         hi, lo = extremes(hi, lo, third, 2)
         for t in range(PACK):
             gather(gathered[3], 3, t)
-        fourth = round_list(gathered[3], "largest1")
-        w34 = quantise(w34_grouped[:].rearrange("p a c -> p (a c)"), 2 * N, "w34")
+        turned_mean = [
+            [keep.tile([P, P, 2], BF16, name=tag, align_bytes=64) for tag in tags]
+            for tags in (("h2", "h3"), ("turned10", "turned11"))
+        ]
+        back = [psum.tile([P, 2, P], F32, name="bank%d" % (1 + b)) for b in range(halves)]
+
+        def turn_back(u, b):
+            nc.scalar.activation(
+                turned_mean[u][b][:].rearrange("v (c i) e -> v c e i", i=4),
+                sums[u][:, b].rearrange("v e (c i) -> v c e i", i=4),
+                COPY,
+                scale=1.0 / D,
+            )
+            pairs = turned_mean[u][b][:].rearrange("v p e -> v (p e)").bitcast(F32)
+            nc.tensor.transpose(back[b][:, u, :], pairs, ident[:])
+
+        turn_back(0, 0)
+        fourth = keep.tile([P, V * PACK], BF16, name="rounded3", align_bytes=64)
+        dst = fourth[:].rearrange("p (c i t) -> p c t i", i=4, t=PACK)
+        src = gathered[3][:].rearrange("p t (c i) -> p c t i", i=4)
+        nc.vector.tensor_copy(dst[:, :VECTOR_SHARE], src[:, :VECTOR_SHARE])
+        nc.scalar.copy(dst[:, VECTOR_SHARE:], src[:, VECTOR_SHARE:])
+        mean_w2 = keep.tile([P, 3, P * PACK], BF16, name="smallest1", align_bytes=64)
+        round_w(mean_w2[:, 0], w_raw[2])
         hi, lo = extremes(hi, lo, fourth, 3)
 
-        mean_w2 = keep.tile([P, 3, P * PACK], BF16, name="h3", align_bytes=64)
-        nc.scalar.copy(
-            mean_w2[:, 0].rearrange("p (c i j) -> p c j i", i=4, j=PACK),
-            w_raw[0][:].rearrange("p j (c i) -> p c j i", i=4),
-        )
+        for u, b in ((0, 1), (1, 0), (1, 1)):
+            turn_back(u, b)
         for b in range(halves):
-            mean_t = keep.tile([P, 2, P, 2], BF16, name="mean_t%d" % b, align_bytes=64)
-            for u in range(2):
-                nc.scalar.activation(
-                    mean_t[:, u].rearrange("v (c i) e -> v c e i", i=4),
-                    sums[b][:, 2 * u : 2 * u + 2].rearrange("v e (c i) -> v c e i", i=4),
-                    COPY,
-                    scale=1.0 / D,
-                )
-            pairs = mean_t[:].rearrange("v u p e -> v (u p e)").bitcast(F32)
-            back = psum.tile([P, 2, P], F32, name="bank%d" % (1 + b))
-            for u in range(2):
-                nc.tensor.transpose(back[:, u, :], pairs[:, u * P : (u + 1) * P], ident[:])
             nc.scalar.copy(
                 mean_w2[:, 1 + b].bitcast(F32).rearrange("p (c i u) -> p c u i", i=2, u=2),
-                back[:].rearrange("p u (c i) -> p c u i", i=2),
+                back[b][:].rearrange("p u (c i) -> p c u i", i=2),
             )
 
         z2 = quantise(hi[:], V, "z2")
@@ -243,8 +260,8 @@ def tile_picked_pna_none_p_kernel(
             cols = slice(b * P, (b + 1) * P)
             acc = psum.tile([P, P], F32, name="bank%d" % (3 + b))
             passes = (
-                (w34, 0, z2, b * P),
-                (w34, N, z3, b * P),
+                (w3q, 0, z2, b * P),
+                (w4q, 0, z3, b * P),
                 (w2_z1, 0, w2_z1, N) if b == 0 else (w2_z1, 0, z1_last, 0),
             )
             for a, (w, m0, zq, v0) in enumerate(passes):

@@ -22,7 +22,6 @@ P = 128
 PACK = 4
 PASSES = K // (P * PACK)
 D = 4
-VECTOR_SHARE = 48
 
 
 def tile_picked_pna_none_p_kernel(
@@ -154,12 +153,14 @@ def tile_picked_pna_none_p_kernel(
 
         turned = [[], []]
 
-        def gather(g, d, t, on_vector=False):
+        def gather(g, d, t, on_vector=False, parts=(0, 1)):
+            targets = slice(parts[0] * P, (parts[-1] + 1) * P)
+            window = h[t][:].indirect(places[d][:, targets.start // 16 : targets.stop // 16])
             if on_vector:
-                nc.vector.tensor_copy(g[:, t, :], h[t][:].indirect(places[d][:]))
+                nc.vector.tensor_copy(g[:, t, targets], window)
             else:
-                nc.scalar.activation(g[:, t, :], h[t][:].indirect(places[d][:]), COPY)
-            for b in range(halves):
+                nc.scalar.activation(g[:, t, targets], window, COPY)
+            for b in parts:
                 nc.tensor.matmul(
                     sums[t // 2][:, b, t % 2, :],
                     lhsT=g[:, t, b * P : (b + 1) * P],
@@ -203,8 +204,9 @@ def tile_picked_pna_none_p_kernel(
             nc.scalar.copy(h[t][:], full[t - 1][:])
             gather(gathered[0], 0, t, on_vector=True)
         gather(gathered[1], 1, 1)
-        gather(gathered[1], 1, 3, on_vector=True)
+        gather(gathered[1], 1, 3, on_vector=True, parts=(0,))
         gather(gathered[1], 1, 2)
+        gather(gathered[1], 1, 3, parts=(1,))
         first = round_list(gathered[0], "rounded0")
         second = round_list(gathered[1], "rounded1")
         w4_grouped = keep.tile([P, N * PACK], BF16, name="g0", align_bytes=64)
@@ -235,11 +237,7 @@ def tile_picked_pna_none_p_kernel(
             nc.tensor.transpose(back[b][:, u, :], pairs, ident[:])
 
         turn_back(0, 0)
-        fourth = keep.tile([P, V * PACK], BF16, name="rounded3", align_bytes=64)
-        dst = fourth[:].rearrange("p (c i t) -> p c t i", i=4, t=PACK)
-        src = gathered[3][:].rearrange("p t (c i) -> p c t i", i=4)
-        nc.vector.tensor_copy(dst[:, :VECTOR_SHARE], src[:, :VECTOR_SHARE])
-        nc.scalar.copy(dst[:, VECTOR_SHARE:], src[:, VECTOR_SHARE:])
+        fourth = round_list(gathered[3], "largest1")
         mean_w2 = keep.tile([P, 3, P * PACK], BF16, name="smallest1", align_bytes=64)
         round_w(mean_w2[:, 0], w_raw[2])
         hi, lo = extremes(hi, lo, fourth, 3)

from contextlib import ExitStack

import concourse.mybir as mybir
from concourse.masks import make_identity

K, T, S, V, H, N = 1024, 2048, 512, 256, 512, 128
FLOPS = 2 * K * H * S + 3 * 2 * H * N * V

F32 = mybir.dt.float32
BF16 = mybir.dt.bfloat16
I32 = mybir.dt.int32
U32 = mybir.dt.uint32
U16 = mybir.dt.uint16
U8 = mybir.dt.uint8
FP8X4 = mybir.dt.float8_e4m3fn_x4
FP4X4 = mybir.dt.float4_e2m1fn_x4
MAX = mybir.AluOpType.max
MIN = mybir.AluOpType.min
COPY = mybir.ActivationFunctionType.Copy

P = 128
PACK = 4
PASSES = K // (P * PACK)
D = 4


def tile_picked_pna_none_p_kernel(
    tc, x_words, x_scales, w1, w2, w3, w4, offs, pos1, pos2, pos3, pos4, out
):
    nc = tc.nc
    with ExitStack() as ctx:
        keep = ctx.enter_context(tc.tile_pool(name="keep", bufs=1))
        psum = ctx.enter_context(tc.psum_pool(name="psum", bufs=1))

        rows = keep.tile([P, T], U8, name="rows", align_bytes=64)
        nc.sync.dma_start(rows[:].bitcast(I32)[0:32], x_scales.bitcast(I32).rearrange("z q c -> q z c"))
        nc.vector.memset(rows[:].bitcast(I32)[32:64], 0)
        nc.vector.memset(rows[:].bitcast(I32)[64:P], 0)
        offsets = keep.tile([P, S // 16], U16, name="offsets")
        nc.sync.dma_start(offsets[:], offs)
        words = [keep.tile([P, T], U16, name="words%d" % z, align_bytes=64) for z in range(PASSES)]
        nc.sync.dma_start(words[0][:].bitcast(I32), x_words[0].bitcast(I32))
        places = []
        for d, pos in enumerate((pos1, pos2, pos3, pos4)):
            place = keep.tile([P, V // 16], U16, name="places%d" % d)
            nc.sync.dma_start(place[:], pos)
            places.append(place)
        w1_rows = w1.rearrange("(z p j) c -> z p j c", p=P, j=PACK)
        w1_first = keep.tile([P, PACK, H], F32, name="w1_first", align_bytes=64)
        nc.sync.dma_start(w1_first[:], w1_rows[0])
        nc.sync.dma_start(words[1][:].bitcast(I32), x_words[1].bitcast(I32))

        ident = keep.tile([P, P], F32, name="ident")
        make_identity(nc, ident[:])

        picked_rows = keep.tile([P, S], U8, name="picked_rows", align_bytes=64)
        nc.vector.tensor_copy(picked_rows[:], rows[:].indirect(offsets[:]))
        x_bytes = keep.tile([P, PASSES * S], U8, name="x_bytes", align_bytes=64)
        nc.vector.memset(x_bytes[:].bitcast(I32), 0)
        for q in range(4):
            nc.sync.dma_start(
                x_bytes[:].bitcast(I32)[32 * q : 32 * q + 4], picked_rows[:].bitcast(I32)[8 * q : 8 * q + 8]
            )
        w1_second = []
        for e, tag in enumerate(("rows", "words0")):
            half = keep.tile([P, PACK, H // 2], F32, name=tag, align_bytes=64)
            w1_second.append(half)
        nc.sync.dma_start(w1_second[0][:], w1_rows[1][:, :, : H // 2])
        x_codes = [keep.tile([P, S], U16, name="x_codes0", align_bytes=64)]
        nc.vector.tensor_copy(x_codes[0][:], words[0][:].indirect(offsets[:]))
        nc.sync.dma_start(w1_second[1][:], w1_rows[1][:, :, H // 2 :])

        spans = ((0, 1), (1, 2), (2, 4))
        w1_codes, w1_scales = {}, {}
        for z in range(PASSES):
            for t0, t1 in spans:
                codes = keep.tile([P, (t1 - t0) * P], U32, name="w1_codes%d%d" % (z, t0), align_bytes=64)
                scales = keep.tile([P, (t1 - t0) * P], U8, name="w1_scales%d%d" % (z, t0), align_bytes=64)
                w1_codes[z, t0, t1], w1_scales[z, t0, t1] = codes[:], scales[:]
                for t in range(t0, t1):
                    cols = slice((t - t0) * P, (t - t0 + 1) * P)
                    w1_codes[z, t], w1_scales[z, t] = codes[:, cols], scales[:, cols]
        h = [keep.tile([P, S], F32, name="h%d" % t, align_bytes=64) for t in range(PACK)]

        def quantise_w1(z, t0, t1, grouped):
            nc.vector.quantize_mx(w1_codes[z, t0, t1].bitcast(FP8X4), w1_scales[z, t0, t1], grouped)

        src = w1_first[:].rearrange("p j (a t r) -> p t a j r", t=PACK, r=2)
        for u in range(2):
            grouped = keep.tile([P, 2 * H], BF16, name="w1_pair%d" % u, align_bytes=64)
            dst = grouped[:].rearrange("p (t a r j) -> p t a j r", t=2, r=2, j=PACK)
            if u == 0:
                nc.vector.tensor_copy(dst[:, 0], src[:, 0])
                nc.vector.tensor_copy(dst[:, 1], src[:, 1])
                quantise_w1(0, 0, 1, grouped[:, 0:H])
                quantise_w1(0, 1, 2, grouped[:, H : 2 * H])
            else:
                nc.scalar.copy(dst, src[:, 2:4])
                quantise_w1(0, 2, 4, grouped[:])
        x_codes.append(keep.tile([P, S], U16, name="w1_pair1", align_bytes=64))
        nc.vector.tensor_copy(x_codes[1][:], words[1][:].indirect(offsets[:]))
        grouped = keep.tile([P, H * PACK], BF16, name="w1_grouped", align_bytes=64)
        dst = grouped[:].rearrange("p (t e a r j) -> p e t a j r", t=PACK, e=2, r=2, j=PACK)
        src = [half[:].rearrange("p j (a t r) -> p t a j r", t=PACK, r=2) for half in w1_second]
        nc.vector.tensor_copy(dst[:, 0, 0:2], src[0][:, 0:2])
        nc.scalar.copy(dst[:, 0, 2:4], src[0][:, 2:4])
        nc.vector.tensor_copy(dst[:, 1, 0], src[1][:, 0])
        nc.vector.tensor_copy(dst[:, 1, 1], src[1][:, 1])
        quantise_w1(1, 0, 1, grouped[:, 0:H])
        nc.scalar.copy(dst[:, 1, 2:4], src[1][:, 2:4])
        quantise_w1(1, 1, 2, grouped[:, H : 2 * H])
        quantise_w1(1, 2, 4, grouped[:, 2 * H : 4 * H])
        banks = 0
        full = []
        for t in range(PACK):
            width = P if t == 0 else S
            for s0 in range(0, S, width):
                entries = slice(s0, s0 + width)
                bank = psum.tile([P, width], F32, name="bank%d" % banks)
                banks += 1
                for z in range(PASSES):
                    nc.tensor.matmul_mx(
                        bank[:],
                        lhsT=w1_codes[z, t].bitcast(FP8X4),
                        lhsT_scale=w1_scales[z, t],
                        rhs=x_codes[z][:, entries].bitcast(FP4X4),
                        rhs_scale=x_bytes[:, z * S + s0 : z * S + s0 + width],
                        start=(z == 0),
                        stop=(z == PASSES - 1),
                    )
                if t > 0:
                    full.append(bank)
                elif (s0 // width) % 2 == 0:
                    nc.vector.tensor_copy(h[t][:, entries], bank[:])
                else:
                    nc.scalar.copy(h[t][:, entries], bank[:])

        w_raw = []
        for tag, w in zip(("picked_rows", "w1_pair0", "words1"), (w3, w4, w2)):
            raw = keep.tile([P, PACK, N], F32, name=tag, align_bytes=64)
            for r in range(2):
                nc.sync.dma_start(raw[r:P:2], w.rearrange("(a t r) n -> r a t n", t=PACK, r=2)[r])
            w_raw.append(raw)

        def quantise(values, width, tag, over=None):
            codes = keep.tile([P, width], U32, name=over or tag, align_bytes=64)
            scales = keep.tile([P, width], U8, name=tag + "_scales", align_bytes=64)
            nc.vector.quantize_mx(codes[:].bitcast(FP8X4), scales[:], values)
            return codes, scales

        halves = V // P
        sums = [psum.tile([P, halves, 2, P], F32, name=("bank7", "bank0")[u]) for u in range(2)]

        turned = [[], []]

        def gather(g, d, t, on_vector=False, parts=(0, 1)):
            targets = slice(parts[0] * P, (parts[-1] + 1) * P)
            window = h[t][:].indirect(places[d][:, targets.start // 16 : targets.stop // 16])
            if on_vector:
                nc.vector.tensor_copy(g[:, t, targets], window)
            else:
                nc.scalar.activation(g[:, t, targets], window, COPY)
            for b in parts:
                nc.tensor.matmul(
                    sums[t // 2][:, b, t % 2, :],
                    lhsT=g[:, t, b * P : (b + 1) * P],
                    rhs=ident[:],
                    is_transpose=True,
                    start=(len(turned[t // 2]) == 0),
                    stop=(len(turned[t // 2]) == 2 * D * halves - 1),
                )
                turned[t // 2].append((d, t, b))

        def round_list(g, tag):
            rounded = keep.tile([P, V * PACK], BF16, name=tag, align_bytes=64)
            nc.vector.tensor_copy(
                rounded[:].rearrange("p (c i t) -> p c t i", i=4, t=PACK),
                g[:].rearrange("p t (c i) -> p c t i", i=4),
            )
            return rounded

        def round_w(dst, raw):
            nc.vector.tensor_copy(
                dst.rearrange("p (c i j) -> p c j i", i=4, j=PACK),
                raw[:].rearrange("p j (c i) -> p c j i", i=4),
            )

        def extremes(largest, smallest, rounded, step):
            hi = keep.tile([P, V * PACK], BF16, name="largest%d" % step, align_bytes=64)
            lo = keep.tile([P, V * PACK], BF16, name="smallest%d" % step, align_bytes=64)
            nc.vector.tensor_tensor(hi[:], largest[:], rounded[:], MAX)
            nc.vector.tensor_tensor(lo[:], smallest[:], rounded[:], MIN)
            return hi, lo

        gathered = [
            keep.tile([P, PACK, V], F32, name=tag, align_bytes=64) for tag in ("g0", "g1", "g2", "w1_pair1")
        ]
        w3_grouped = keep.tile([P, N * PACK], BF16, name="w1_codes10", align_bytes=64)
        round_w(w3_grouped[:], w_raw[0])
        gather(gathered[0], 0, 0, on_vector=True)
        gather(gathered[1], 1, 0)
        gather(gathered[2], 2, 0, on_vector=True)
        for t in range(1, PACK):
            nc.scalar.copy(h[t][:], full[t - 1][:])
            gather(gathered[0], 0, t, on_vector=True)
        gather(gathered[1], 1, 1)
        gather(gathered[1], 1, 3, on_vector=True, parts=(0,))
        gather(gathered[1], 1, 2)
        gather(gathered[1], 1, 3, parts=(1,))
        first = round_list(gathered[0], "rounded0")
        second = round_list(gathered[1], "rounded1")
        w4_grouped = keep.tile([P, N * PACK], BF16, name="g0", align_bytes=64)
        round_w(w4_grouped[:], w_raw[1])
        hi, lo = extremes(first, first, second, 1)
        for t in range(1, PACK):
            gather(gathered[2], 2, t)
        third = round_list(gathered[2], "g1")
        w3q = quantise(w3_grouped[:], N, "w3q", "rounded1")
        w4q = quantise(w4_grouped[:], N, "w4q", "rounded0")
        hi, lo = extremes(hi, lo, third, 2)
        for t in range(PACK):
            gather(gathered[3], 3, t)
        turned_mean = [
            [keep.tile([P, P, 2], BF16, name=tag, align_bytes=64) for tag in tags]
            for tags in (("h2", "h3"), ("turned10", "turned11"))
        ]
        back = [psum.tile([P, 2, P], F32, name="bank%d" % (1 + b)) for b in range(halves)]

        def turn_back(u, b):
            nc.scalar.activation(
                turned_mean[u][b][:].rearrange("v (c i) e -> v c e i", i=4),
                sums[u][:, b].rearrange("v e (c i) -> v c e i", i=4),
                COPY,
                scale=1.0 / D,
            )
            pairs = turned_mean[u][b][:].rearrange("v p e -> v (p e)").bitcast(F32)
            nc.tensor.transpose(back[b][:, u, :], pairs, ident[:])

        turn_back(0, 0)
        fourth = round_list(gathered[3], "largest1")
        mean_w2 = keep.tile([P, 3, P * PACK], BF16, name="smallest1", align_bytes=64)
        round_w(mean_w2[:, 0], w_raw[2])
        hi, lo = extremes(hi, lo, fourth, 3)

        for u, b in ((0, 1), (1, 0), (1, 1)):
            turn_back(u, b)
        for b in range(halves):
            nc.scalar.copy(
                mean_w2[:, 1 + b].bitcast(F32).rearrange("p (c i u) -> p c u i", i=2, u=2),
                back[b][:].rearrange("p u (c i) -> p c u i", i=2),
            )

        z2 = quantise(hi[:], V, "z2")
        z3 = quantise(lo[:], V, "z3")
        w2_z1 = quantise(mean_w2[:, 0:2].rearrange("p a c -> p (a c)"), N + P, "w2_z1", "largest2")
        z1_last = quantise(mean_w2[:, 2], P, "z1_last", "smallest2")
        for b in range(halves):
            cols = slice(b * P, (b + 1) * P)
            acc = psum.tile([P, P], F32, name="bank%d" % (3 + b))
            passes = (
                (w3q, 0, z2, b * P),
                (w4q, 0, z3, b * P),
                (w2_z1, 0, w2_z1, N) if b == 0 else (w2_z1, 0, z1_last, 0),
            )
            for a, (w, m0, zq, v0) in enumerate(passes):
                nc.tensor.matmul_mx(
                    acc[:],
                    lhsT=w[0][:, m0 : m0 + N].bitcast(FP8X4),
                    lhsT_scale=w[1][:, m0 : m0 + N],
                    rhs=zq[0][:, v0 : v0 + P].bitcast(FP8X4),
                    rhs_scale=zq[1][:, v0 : v0 + P],
                    start=(a == 0),
                    stop=(a == 2),
                )
            result = keep.tile([P, P], F32, name="result%d" % b)
            if b == 0:
                nc.scalar.copy(result[:], acc[:])
            else:
                nc.vector.tensor_copy(result[:], acc[:])
            nc.sync.dma_start(out[:, cols], result[:])
